import numpy as np, ml_dtypes
CORES = [36,164,52,180,100,228,116,244]
N = 8
BF = ml_dtypes.bfloat16
V, M, CAP, RO = 1024, 2, 48, 2
def phone(rng):
    loc = rng.choice(np.array([0.0, 0.2, 0.5, 0.8]), (N, 8, 1, 1))
    far = rng.integers(0, N * V, (N, 8, 16, V)); near = rng.integers(0, V, (N, 8, 16, V)) + V * np.arange(N)[:, None, None, None]
    return np.where(rng.random((N, 8, 16, V)) < loc, near, far)
def lore(rng):
    share = rng.choice(np.array([0.0, 0.0, 0.0625, 0.125, 0.3]), (N, 8, 1, V))
    return np.where(rng.random((N, 8, 16, V)) < share, rng.integers(1, 256, (N, 8, 16, V)), 0)
def dense(rng, sec, tel, g, d, lean):
    x = np.arange(N * V).reshape(N, 1, V); goal = x[:, 0] ^ 1; h = V // 2; i = 0
    run = 2 * ((64 * int(rng.integers(0, V // 128)) + rng.permutation((N - 1) * CAP)) % h)
    for r in range(N):
        if r == d: continue
        goal[r, 2 * rng.permutation(h)[:CAP]] = d * V + run[i:i + CAP]; i += CAP
    s = rng.integers(0, 256, (N, 16, V)); a, b = (int(k) for k in rng.permutation(16)[:2])
    s[:, a, 0::2] = rng.integers(0, 51, (N, h)); s[d, a, 0::2] = rng.integers(51, 101, h); s[:, a, 1::2] = rng.integers(101, 256, (N, h))
    s[:, b, 0::2] = rng.integers(128, 256, (N, h)); s[:, b, 1::2] = rng.integers(0, 128, (N, h))
    sec[:, g] = s
    if lean:
        row = rng.integers(0, 16, (N, 1, V)); t = np.where(np.arange(16)[None, :, None] == row, goal[:, None, :], x)
        if M == 2: t[:, :, 1::2] = tel[:, g, :, 1::2]
        tel[:, g] = t
    else: tel[:, g] = goal[:, None, :]
def pack(sec, tel):
    return {"sec": np.ascontiguousarray(sec.reshape(N, 128, V)).astype(np.float32).astype(BF), "tel": np.ascontiguousarray(tel.reshape(N, 128, V)).astype(np.int32)}
def setup_inputs(rng):
    tel, sec = phone(rng), lore(rng); me = np.arange(N * V).reshape(N, 1, 1, V)
    tel = np.where(rng.random((N, 8, 1, V)) < 0.03, me, tel); sec = np.where(rng.random((N, 8, 1, V)) < 0.004, 255, sec)
    return pack(sec, tel)
def setup_inputs_room(rng):
    b = rng.integers(0, 100, (8, 16)); sec = np.broadcast_to(b[None, :, :, None], (N, 8, 16, V)).copy()
    o = np.argsort(rng.random((N, 8, V)), axis=-1); kn, non = o[:, :, :16], o[:, :, 16:]
    s = rng.integers(0, N, (N, 8, 16, V)); tel = s * V + non[s, np.arange(8)[None, :, None, None], rng.integers(0, V - 16, (N, 8, 16, V))]
    for q in range(N):
        for g in range(8):
            sec[q, g][:, kn[q, g]] = b[g][:, None] + rng.integers(1, 100, (16, 16))
            cal = non[q, g][non[q, g] % M == 0]; pos = 0
            for d in range(1, N + 1):
                z = (q + d) % N; n = int(rng.choice(np.array([0, 1, CAP - 1, CAP, CAP + 1, CAP + 8])))
                if q == 0 and d == 1: n = (CAP, CAP + 1, CAP - 1, CAP + 8, 1, 0, CAP, CAP + 1)[g]
                if d == N: n = 20
                tel[q, g, rng.integers(0, 16, n), cal[pos:pos + n]] = z * V + kn[z, g, rng.integers(0, 16, n)]
                pos += n
    return pack(sec, tel)
def setup_inputs_ties(rng):
    tel = phone(rng); tel[:, :, 8:] = tel[:, :, 7::-1]
    sec = (rng.random((N, 8, 16, V)) < rng.choice(np.array([0.05, 0.2, 0.5]), (N, 8, 1, V))).astype(np.int64)
    sec[:, ::2] *= 255
    m = rng.random((N, 4, 16, V)) < 0.1
    tel[:, 1::2] = np.where(m, rng.choice(np.array([0, V - 1, V, N * V - 1]), m.shape), tel[:, 1::2])
    return pack(sec, tel)
def setup_inputs_crowd(rng):
    tel, sec = phone(rng), lore(rng); x = np.arange(N * V).reshape(N, 1, V); o = rng.permutation(8)
    for g in o[:3]: sec[:, g] = rng.integers(0, 256, (N, 16, V))
    tel[:, o[0]] = (x + M) % (N * V); tel[:, o[1]] = x ^ M; tel[:, o[2]] = (x + V) % (N * V)
    sec[:, o[3:5]] = np.minimum(sec[:, o[3:5]], 200)
    star = int(rng.choice(np.array([0, V - 1, N * V - V, N * V - 1]))); tel[:, o[3], int(rng.integers(0, 16))] = star; sec[star // V, o[3], :, star % V] = 255
    place = rng.choice(np.array([0, V - 1]), N)
    tel[:, o[4], int(rng.integers(0, 16))] = (np.arange(N) * V + place)[rng.integers(0, N, (N, V))]
    for q in range(N): sec[q, o[4], :, place[q]] = 255
    dense(rng, sec, tel, int(o[5]), N - 1, False)
    dense(rng, sec, tel, int(o[6]), int(rng.integers(0, N - 1)), True)
    return pack(sec, tel)
def setup_inputs_alike(rng):
    tel, sec = phone(rng), lore(rng); x = np.arange(N * V).reshape(N, 1, V); o = rng.permutation(8)
    sec[:, o[0]] = rng.integers(0, 256, (1, 16, 1))
    sec[:, o[1]] = 0; sec[int(rng.integers(0, N)), o[1]] = 255
    one = int(rng.choice(np.array([0, N * V - 1]))); sec[:, o[2]] = 0; sec[one // V, o[2], int(rng.integers(0, 16)), one % V] = int(rng.integers(1, 256)); tel[:, o[2], 15] = one
    tel[:, o[3], 1:] = x
    sec[:, o[4]] = rng.integers(254, 256, (N, 16, V))
    sec[:, o[5]] = np.where(rng.random((N, 1, V)) < 0.5, 0, rng.integers(230, 256, (N, 16, V)))
    z = rng.integers(-40, 41, (N, 8, V)); s = 128 + np.concatenate([z, -z], axis=1); s[:, int(rng.integers(0, 16))] += rng.integers(-1, 2, (N, V))
    sec[:, o[6]] = np.where(rng.random((N, 1, V)) < 0.5, 0, s)
    return pack(sec, tel)
def setup_inputs_spread(rng):
    sec = np.floor(np.exp2(8 * rng.random((N, 8, 1, V))) * np.exp2(-4 * rng.random((1, 8, 16, 1))) * rng.random((N, 8, 16, V))).astype(np.int64)
    sec = np.where(rng.random((N, 8, 16, V)) < rng.random((N, 8, 1, V)), np.minimum(sec, 255), 0)
    o = np.argsort(rng.random((8, N * V)), axis=-1); k = np.minimum((N * V * rng.random((N, 8, 16, V)) ** 3).astype(np.int64), N * V - 1)
    return pack(sec, o[np.arange(8)[None, :, None, None], k])
def check_inputs(d):
    bad = []; s = np.asarray(d["sec"]).astype(np.float32); a = np.asarray(d["tel"])
    if not np.all((s >= 0) & (s <= 255) & (s == np.floor(s))): bad.append("sec: whole numbers from 0 to 255")
    if np.min(a) < 0 or np.max(a) > N * V - 1: bad.append("range of tel")
    return bad
def world(a):
    return np.ascontiguousarray(a.astype(np.int64).reshape(N, 8, 16, V).transpose(1, 2, 0, 3)).reshape(8, 16, N * V)
def ranks(a):
    return np.ascontiguousarray(a.reshape(8, 16, N, V).transpose(2, 0, 1, 3)).reshape(N, 128, V).astype(np.float32)
def reference(sec, tel):
    S, T = world(sec.astype(np.float32)), world(tel)
    for t in range(RO):
        x = (np.arange(N)[:, None] * V + np.arange(t % M, V, M)[None, :]).reshape(-1)
        Sn, Tn = S.copy(), T.copy()
        for g in range(8):
            tl = T[g][:, x]; gain = np.zeros(tl.shape, np.int64)
            for f in range(16): gain += np.maximum(S[g, f][tl] - S[g, f][x][None, :], 0)
            row = np.argmax(gain, axis=0)
            c = np.take_along_axis(tl, row[None, :], 0)[0]; call = np.max(gain, axis=0) > 0
            through = call.reshape(N, -1)
            for s in range(N):
                flag = (call & (c // V == s)).reshape(N, -1); count = np.add.accumulate(flag.astype(np.int64), axis=1)
                through = through & (~flag | (count <= CAP) | (np.arange(N)[:, None] == s))
            w = np.flatnonzero(through.reshape(-1)); u, first = np.unique(c[w], return_index=True); w = w[first]; v = x[w]
            Sn[g][:, v] = np.maximum(S[g][:, v], S[g][:, u])
            Sn[g][:, u] = np.maximum(Sn[g][:, u], S[g][:, v])
            Tn[g][:, v] = np.where(gain[:, w] == 0, T[g][:, u], T[g][:, v])
            Tn[g, t, u] = v
        S, T = Sn, Tn
        if t < RO - 1: T = np.roll(Tn, 1, axis=0)
    return {"ysec": ranks(S).astype(BF), "ytel": ranks(T)}

@@ -1,0 +1,611 @@
+import math
+import numpy as np
+from concourse.bass import DstId, RemoteDMATransfer
+from concourse.mybir import AluOpType, AxisListType, ActivationFunctionType
+
+N = 8
+NPE = 4
+B = 2.4
+LNB = math.log(B)
+W0 = math.exp(43.7)
+F32, BF, I32, U16 = "float32", "bfloat16", "int32", "uint16"
+
+
+def sb(cols, dtp):
+    return ("sbuf", [128] + (list(cols) if isinstance(cols, (list, tuple)) else [cols]), dtp)
+
+
+def slots(cols, dtp):
+    return ("dram", [N, 128, cols], dtp)
+
+
+SCRATCH = {
+    "so": slots(128, BF), "si": slots(128, BF), "eso": slots(128, BF), "esi": slots(128, BF),
+    "toe": slots(64, U16), "too": slots(64, U16), "tie": slots(64, U16), "tio": slots(64, U16),
+    "eon": slots(64, U16), "eoc": slots(64, U16), "ein": slots(64, U16), "eic": slots(64, U16),
+    "tab": sb(8192, BF), "rep": sb(8192, BF), "mx": sb(8192, BF), "iw": sb(8192, F32),
+    "ws0": sb(1376, BF), "ws1": sb(1376, BF), "ws2": sb(1024, BF),
+    "wt": sb(1376, F32), "ww": sb(1376, F32), "tn": sb(1024, F32), "t32": sb(1024, I32), "tu": sb(1024, U16),
+    "lt0": sb(512, U16), "th0": sb(512, U16), "lt1": sb(512, U16), "th1": sb(512, U16),
+    "un0": sb(512, U16), "uc0": sb(512, U16), "un1": sb(512, U16), "uc1": sb(512, U16), "yn": sb(512, U16), "yc": sb(512, U16),
+    "sw": sb(912, BF), "idw": sb(912, F32), "tp": sb(512, F32), "tc": sb(512, F32),
+    "iob": sb(256, BF), "ioa": sb(128, BF), "iog": sb(128, BF), "pi": sb(8, I32), "pc": sb(16, F32),
+    "iib": sb(256, BF), "nib": sb(128, BF), "iif": sb(256, F32), "ztf": sb(240, F32), "one8": sb(8, BF), "negb": sb(128, BF),
+    "tri": sb(128, BF), "ones": sb(128, BF), "selr": sb(128 * max(NPE, 1), BF), "tile": sb(128, BF), "m8": sb(8, F32),
+    "wrow": sb(128, F32), "wtmp": sb(128, F32), "wz": sb(128, F32), "wcol": sb(8, F32), "cst": sb(12, F32), "off": sb(12, F32),
+    "l0": sb(2, F32), "ag": sb(512, F32), "rs": sb(512, F32), "rs8": sb(256, F32),
+    "rn": sb(32, F32), "rni": sb(32, I32), "mn": sb(32, F32),
+    "bl24": sb(24, F32), "rl": sb(2, U16), "ctmp": sb(16, F32), "ctmi": sb(16, I32), "rowm": sb(8, F32),
+    "k1": sb(512, F32), "rec": sb(512, F32), "k2": sb(512, F32), "zz": sb(512, BF),
+    "di": sb(192, I32), "df": sb(160, F32), "sm": sb(768, F32), "ki": sb(96, I32),
+    "oh": sb(256, BF), "pm": sb(256, F32), "pn": sb(256, F32),
+    "aa": sb(4096, BF), "bp": sb(288, BF), "dl": sb(2048, BF), "bl": sb(2048, BF),
+    "ee": sb([4, 8, 8], F32), "li": sb(32, U16), "cps": sb([8, 9], F32),
+    "ar": sb(3072, BF), "bq": sb(1536, BF), "um": sb(64, F32), "lud": sb(32, U16), "lidd": sb(32, U16),
+    "lid": sb(24, U16), "gs": sb(336, BF), "gt": sb(336, F32), "sid": sb(336, F32), "fl": sb(336, BF),
+    "lc": sb(256, F32), "lg": sb(768, F32), "es": sb(768, F32), "va": sb(768, F32), "vs": sb(768, F32),
+    "qi": sb(64, I32), "sq": sb(512, F32), "lk": sb(64, U16),
+    "ff": sb(512, F32), "xs": sb(512, BF), "dt": sb(512, F32), "hn": sb(512, F32), "hc": sb(512, F32),
+}
+for _k in range(8):
+    SCRATCH["p%d" % _k] = ("psum", [128, 512], F32)
+SEMAPHORES = ["qv", "qa", "qp", "qg", "ls", "lt", "os", "oe", "oo", "de", "do", "as1", "ae1", "ao1", "sent", "ns", "ne", "no",
+              "tb0", "tb1", "an2", "ac2", "es", "en", "ec", "oen", "oec", "aes", "aen", "aec", "ys", "yt", "oes", "ln", "lc"]
+
+A = AluOpType
+AF = ActivationFunctionType
+
+
+def program(g, core, T, topo, rank):
+    S = np.s_
+    eng = {"v": g.vector, "a": g.scalar, "p": g.tensor, "g": g, "s": g.sync}
+    qsem = {"v": "qv", "a": "qa", "p": "qp", "g": "qg"}
+    cnt = {}
+    seen = {q: {} for q in eng}
+    toks = [None]
+    wr, rd = {}, {}
+    bank = {}
+
+    def shape(name):
+        return SCRATCH[name][1] if name in SCRATCH else list(T[name].shape)
+
+    def psum(name):
+        return name in SCRATCH and SCRATCH[name][0] == "psum"
+
+    def known(name):
+        if name not in wr:
+            wr[name] = np.zeros(shape(name), np.int32)
+            rd[name] = {}
+
+    def ap(r):
+        if not isinstance(r, tuple):
+            return r
+        if r[0] == "ind":
+            return ap(r[1]).indirect(ap(r[2]))
+        return T[r[0]][r[1]]
+
+    def flat(rs):
+        out = []
+        for r in rs:
+            if isinstance(r, tuple):
+                out += [r[1], r[2]] if r[0] == "ind" else [r]
+        return out
+
+    def wait(q, sem, val):
+        if seen[q].get(sem, 0) < val:
+            eng[q].wait_ge(T.sem[sem], val)
+            seen[q][sem] = val
+
+    def deps(q, reads, writes):
+        need = set()
+        for name, idx in reads + writes:
+            known(name)
+            if psum(name):
+                for q2, tk in bank.get(name, {}).items():
+                    if q2 != q:
+                        need.add(tk)
+                if q == "p":
+                    continue
+            need.update(np.unique(wr[name][idx]).tolist())
+        for name, idx in writes:
+            if q == "p":
+                continue
+            for arr in rd[name].values():
+                need.update(np.unique(arr[idx]).tolist())
+        best = {}
+        for tk in need:
+            if tk:
+                sem, val = toks[tk]
+                best[sem] = max(best.get(sem, 0), cnt[sem] if val is None else val)
+        for sem in sorted(best):
+            wait(q, sem, best[sem])
+
+    def mark(q, tk, reads, writes):
+        for name, idx in reads:
+            if q not in rd[name]:
+                rd[name][q] = np.zeros(shape(name), np.int32)
+            rd[name][q][idx] = tk
+        for name, idx in writes:
+            wr[name][idx] = tk
+        for name, idx in reads + writes:
+            if psum(name):
+                bank.setdefault(name, {})[q] = tk
+
+    def op(q, fn, outs, ins):
+        reads, writes = flat(ins), flat(outs)
+        deps(q, reads, writes)
+        sem = qsem[q]
+        fn().then_inc(T.sem[sem], 1)
+        cnt[sem] = cnt.get(sem, 0) + 1
+        toks.append((sem, cnt[sem]))
+        mark(q, len(toks) - 1, reads, writes)
+
+    def dma(q, sem, out, in_):
+        deps(q, [in_], [out])
+        eng[q].dma_start(ap(out), ap(in_)).then_inc(T.sem[sem], 16)
+        cnt[sem] = cnt.get(sem, 0) + 16
+        toks.append((sem, None))
+        mark("d" + sem, len(toks) - 1, [in_], [out])
+
+    def landed(sem, n, refs):
+        cnt[sem] = n
+        toks.append((sem, n))
+        for name, idx in refs:
+            known(name)
+            wr[name][idx] = len(toks) - 1
+
+    def c(name, a, b=None, step=None):
+        return (name, S[:, a:(a + 1 if b is None else b):step])
+
+    def ind(win, off):
+        return ("ind", win, off)
+
+    def cp(out, in_):
+        op("v", lambda: g.vector.tensor_copy(ap(out), ap(in_)), [out], [in_])
+
+    def tt(out, a, b, o):
+        op("v", lambda: g.vector.tensor_tensor(ap(out), ap(a), ap(b), o), [out], [a, b])
+
+    def ts(out, a, s1, o1, s2=None, o2=None):
+        if o2 is None:
+            op("v", lambda: g.vector.tensor_scalar(ap(out), ap(a), ap(s1), None, o1), [out], [a, s1])
+        else:
+            op("v", lambda: g.vector.tensor_scalar(ap(out), ap(a), ap(s1), ap(s2), o1, o2), [out], [a, s1, s2])
+
+    def scan(out, d0, d1, init, o0, o1):
+        op("v", lambda: g.vector.tensor_tensor_scan(ap(out), ap(d0), ap(d1), init, o0, o1), [out], [d0, d1])
+
+    def ms(out, val):
+        op("v", lambda: g.vector.memset(ap(out), val), [out], [])
+
+    def red(out, in_):
+        op("v", lambda: g.vector.tensor_reduce(ap(out), ap(in_), AxisListType.X, A.add), [out], [in_])
+
+    def act(out, in_, f, bias=None, scale=None):
+        kw = {}
+        if bias is not None:
+            kw["bias"] = ap(bias)
+        if scale is not None:
+            kw["scale"] = ap(scale)
+        op("a", lambda: g.scalar.activation(ap(out), ap(in_), f, **kw), [out], [in_, bias, scale])
+
+    def mm(out, l, r, start=True, stop=True):
+        op("p", lambda: g.tensor.matmul(ap(out), ap(l), ap(r), start, stop), [out], [l, r])
+
+    def iota(out, pat, base, cm, small=True):
+        if small:
+            op("g", lambda: g.iota(ap(out), pat, base, cm, allow_small_or_imprecise_dtypes=True), [out], [])
+        else:
+            op("g", lambda: g.iota(ap(out), pat, base, cm), [out], [])
+
+    others = [(rank + d) % N for d in range(1, N)]
+
+    def swap(src, dst, rsem):
+        deps("g", [(src, S[p]) for p in others], [])
+        trs = []
+        for k, p in enumerate(others):
+            rid, pid = topo.addr(T.cores[p], core)
+            trs.append(RemoteDMATransfer(dst_ids=[DstId(rid=rid, pnc=pid)], dma_engine_mask=1 << topo.engines(core, T.cores[p])[k],
+                                         remote_sem=T.sem[rsem], src=T[src][p], dst=T[dst][rank]))
+        g.remote_dma_fused(trs, local_sem=T.sem.sent)
+        cnt["sent"] = cnt.get("sent", 0) + len(trs)
+
+    def hand_on(src, dst, rsem):
+        nxt = T.cores[(rank + 1) % N]
+        rid, pid = topo.addr(nxt, core)
+        deps("g", [(src, S[:])], [])
+        g.remote_dma(T[dst][:], T[src][:], T.sem[rsem], T.sem.sent, pid, rid, topo.mask(core, nxt))
+        cnt["sent"] += len(topo.engines(core, nxt))
+
+    mine = S[16 * rank:16 * rank + 16]
+    dma("s", "ls", ("so", S[:]), ("sec", S[:]))
+    dma("a", "lt", ("t32", S[:]), ("tel", S[:]))
+    dma("s", "os", ("si", S[rank]), ("sec", S[mine, :]))
+    iota(c("pi", 0), [[0, 1]], 0, 1, False)
+    iota(c("iob", 0, 256), [[1, 256]], 0, 0)
+    iota(c("ioa", 0, 128), [[0, 8], [1, 16]], 0, 0)
+    swap("so", "si", "as1")
+    cp(c("tu", 0, 512), c("t32", 0, 1024, 2))
+    dma("s", "de", ("toe", S[:]), c("tu", 0, 512))
+    dma("a", "oe", ("tie", S[rank]), ("tu", S[mine, 0:512]))
+    cp(c("tu", 512, 1024), c("t32", 1, 1024, 2))
+    dma("s", "do", ("too", S[:]), c("tu", 512, 1024))
+    dma("a", "oo", ("tio", S[rank]), ("tu", S[mine, 512:1024]))
+    iota(c("iog", 0, 128), [[1, 8], [0, 16]], 0, 0)
+    iota(c("rni", 0, 32), [[0, 4], [1, 8]], 0, 0, False)
+    iota(c("mn", 0, 32), [[128, 4], [0, 8]], -256, 1)
+    iota(c("bl24", 0, 24), [[1024, 8], [0, 3]], 512, 0)
+    iota(c("ctmi", 0, 2), [[16, 2]], 0, 0, False)
+    iota(c("off", 0, 8), [[128, 4], [32, 2]], 0, 0)
+    iota(c("off", 8, 12), [[96, 4]], 0, 0)
+    swap("toe", "tie", "ae1")
+    swap("too", "tio", "ao1")
+    iota(c("idw", 0, 512), [[2, 512]], 0, 0)
+    iota(c("iw", 0, 8192), [[1, 8192]], 0, 0)
+    for sem, name in (("as1", "si"), ("ae1", "tie"), ("ao1", "tio"), ("aes", "esi"), ("aen", "ein"), ("aec", "eic")):
+        landed(sem, N - 1, [(name, S[p]) for p in others])
+    for sem, name in (("an2", "lt1"), ("ac2", "th1")):
+        landed(sem, len(topo.engines(T.cores[(rank - 1) % N], core)), [(name, S[:])])
+
+    ts(c("pi", 1), c("pi", 0), 15, A.bitwise_and)
+    ts(c("pi", 2), c("pi", 0), 4, A.arith_shift_right)
+    cp(c("pc", 0, 3), c("pi", 0, 3))
+    P, PA, PG = c("pc", 0), c("pc", 1), c("pc", 2)
+    G16, G48, G48N, G1K, BT, A112, TINY, TINY2, ONE, NTHR, NEG1, NW, NBT = [c("pc", k) for k in range(3, 16)]
+    ts(c("tile", 0, 128), c("ioa", 0, 128), PA, A.is_equal)
+    ts(c("m8", 0, 8), c("iob", 0, 8), PG, A.is_equal)
+    for k in range(NPE):
+        ts(c("selr", 128 * k, 128 * k + 128), c("tile", 0, 128), c("m8", k), A.mult)
+    ts(G16, PG, 16.0, A.mult)
+    ts(G48, PG, 48.0, A.mult, -0.5, A.add)
+    ts(G48N, PG, -48.0, A.mult, 384.0, A.add)
+    ts(G1K, PG, 1024.0, A.mult)
+    ts(BT, PA, 8192.0, A.mult, 8192.0, A.add)
+    ts(A112, PA, 112.0, A.add)
+    ts(NBT, PA, -8192.0, A.mult, -8192.0, A.add)
+    ms(TINY, math.exp(-43.0))
+    ms(TINY2, 0.6 * W0 / B ** 95)
+    ms(ONE, 1.0)
+    ms(NTHR, 39.62)
+    ms(NEG1, -1.0)
+    for h in range(2):
+        ts(c("iib", 128 * h, 128 * h + 128), c("iob", 0, 128), P, A.is_equal)
+    ts(c("nib", 0, 128), c("iob", 0, 128), P, A.is_equal, -1.0, A.mult)
+    cp(c("iif", 0, 256), c("iib", 0, 256))
+    ts(c("ztf", 0, 240), c("iob", 0, 240), A112, A.is_equal)
+    ts(c("one8", 0, 8), c("m8", 0, 8), 16.0, A.mult)
+    ts(c("tri", 0, 128), c("iob", 0, 128), P, A.is_ge)
+    ms(c("ones", 0, 128), 1.0)
+    ms(c("wtmp", 0, 128), 1.0 / B)
+    ms(c("wz", 0, 128), 0.0)
+    scan(c("wrow", 0, 128), c("wtmp", 0, 128), c("wz", 0, 128), W0 * B, A.mult, A.add)
+    act(c("l0", 0), c("wrow", 0), AF.Ln)
+    tt(c("wtmp", 0, 96), c("wrow", 0, 96), c("tile", 0, 96), A.mult)
+    tt(c("wz", 0, 128), c("wrow", 0, 128), c("iib", 0, 128), A.mult)
+    for j in range(6):
+        red(c("wcol", j), c("wtmp", 16 * j, 16 * j + 16))
+    red(c("wcol", 6), c("wz", 0, 128))
+    ms(c("ag", 0, 512), 1.0)
+    ms(c("rs", 0, 512), 1.0)
+    ms(c("rs8", 0, 256), 1.0)
+    ts(NW, c("wcol", 6), -1.0, A.mult)
+    ms(c("ag", 0, 512, 16), -1048576.0)
+    ms(c("rs", 0, 512, 16), 0.0)
+    ms(c("rs8", 0, 256, 8), 0.0)
+    ms(c("idw", 896, 912), -1.0)
+    ms(c("sw", 896, 912), 0.0)
+    ms(c("ww", 1360, 1376), -1.0)
+    ms(c("wt", 1360, 1376), 0.0)
+    ms(c("ws0", 1360, 1376), 0.0)
+    ms(c("ws1", 1360, 1376), 0.0)
+    ms(c("um", 0, 64), 0.0)
+    ts(c("rowm", 0, 2), c("iob", 0, 2), PA, A.is_equal)
+    ts(c("l0", 1), c("l0", 0), -1.0 / (2048 * LNB), A.mult, -0.32 / 2048, A.add)
+    ts(c("rowm", 2, 4), c("rowm", 0, 2), -1.0, A.mult)
+    ts(c("negb", 0, 128), c("iog", 0, 128), PG, A.is_equal, -16.0, A.mult)
+    ts(c("rowm", 4, 6), c("rowm", 2, 4), 1.0, A.add)
+    ts(c("rn", 0, 32), c("rni", 0, 32), 1.0, A.add)
+    ts(c("cst", 0, 12), c("off", 0, 12), -1.0 / 2048, A.mult, c("l0", 1), A.add)
+    ts(c("ctmp", 0, 2), c("ctmi", 0, 2), PA, A.add, 20.0, A.min)
+    ts(c("ctmp", 2, 4), c("ctmp", 0, 2), -1.0, A.add, 1.0 / 3, A.mult)
+    cp(c("ctmi", 2, 4), c("ctmp", 2, 4))
+    ts(c("ctmp", 4, 6), c("ctmi", 2, 4), -3.0, A.mult)
+    tt(c("ctmp", 4, 6), c("ctmp", 4, 6), c("ctmp", 0, 2), A.add)
+    ts(c("ctmp", 6, 8), c("ctmi", 2, 4), -1.0, A.mult, 7.0, A.add)
+    ts(c("ctmi", 4, 6), c("ctmp", 6, 8), PG, A.add)
+    ts(c("ctmi", 6, 8), c("ctmi", 4, 6), 7, A.bitwise_and)
+    ts(c("ctmp", 8, 10), c("ctmi", 6, 8), 3.0, A.mult)
+    tt(c("ctmp", 8, 10), c("ctmp", 8, 10), c("ctmp", 4, 6), A.add)
+    cp(c("rl", 0, 2), c("ctmp", 8, 10))
+    ts(c("idw", 0, 512), c("idw", 0, 512), G1K, A.add)
+
+    def sm(k, n=32):
+        return c("sm", 32 * k, 32 * k + n)
+
+    def sq(k):
+        return c("sq", 64 * k, 64 * k + 64)
+
+    def repeat(J):
+        for i in range(16):
+            cp(c("rep", 2048 * J + i, 2048 * J + 2048, 16), c("sw", 128 * J, 128 * J + 128))
+
+    def gains(J):
+        pb, o = ("p0", 128 * J) if J < 3 else ("p1", 0)
+        if J:
+            mm(c(pb, o, o + 128), c("sw", 128 * J, 128 * J + 128), c("negb", 0, 128), True, False)
+        for i in range(16):
+            if J:
+                mm(c(pb, o + i, o + 128, 16), c("mx", 2048 * J + i, 2048 * J + 2048, 16), c("one8", 0, 8), False, i == 15)
+            else:
+                mm(c(pb, i, 128, 16), c("rep", 128 * i, 128 * i + 128), c("one8", 0, 8))
+
+    def table(t):
+        ws = "ws%d" % t
+        if t == 0:
+            dma("s", "ns", c(ws, 0, 1024), ("si", S[:]))
+        n = 0
+        for r in range(NPE, N):
+            for q in range(N):
+                src = ("si", S[r]) if t == 0 else (ws, S[16 * r:16 * r + 16, 0:1024])
+                dma("sa"[n % 2], "tb%d" % t, ("tab", S[16 * q:16 * q + 16, 1024 * r:1024 * r + 1024]), src)
+                n += 1
+        if t == 0:
+            dma("s", "ne", ("lt0", S[:]), ("tie", S[:]))
+            dma("s", "no", ("th0", S[:]), ("tio", S[:]))
+        for k in range(2 * NPE):
+            pb = "p%d" % (4 + k % 2)
+            mm(c(pb, 0, 512), c("selr", 128 * (k // 2), 128 * (k // 2) + 128), c(ws, 512 * (k % 2), 512 * (k % 2) + 512))
+            act(c("tab", 512 * k, 512 * k + 512), c(pb, 0, 512), AF.Copy)
+        cp(c("sw", 0, 512), c(ws, t, 1024, 2))
+        repeat(1)
+
+    def turn(pb, ident, src):
+        for d in range(1, 8):
+            o = 48 * (d - 1)
+            mm(c(pb, o, o + 48), c(ident, 16 * d, 16 * d + 128), c(src, o, o + 48))
+
+    table(0)
+    repeat(2)
+    repeat(3)
+    for t in range(2):
+        ws, wn, lt, th_ = "ws%d" % t, "ws%d" % (t + 1), "lt%d" % t, "th%d" % t
+        ts(c("tp", 0, 512), c(lt, 0, 512), BT, A.add)
+        for JJ in range(4):
+            mm(c("p2", 128 * JJ, 128 * JJ + 128), c("tp", 128 * JJ, 128 * JJ + 128), c("iif", 0, 128))
+        for h in range(2):
+            act(c("mx", 1024 * h, 1024 * h + 1024), ind(c("tab", 0, 8192), c(lt, 64 * h, 64 * h + 64)), AF.Copy)
+        if t:
+            for i in range(16):
+                act(c("rep", 6144 + i, 8192, 16), c("sw", 384, 512), AF.Copy)
+        act(c("tc", 0, 512), c("tp", 0, 512), AF.Identity, bias=NBT)
+        act(c("wt", t, 1024, 2), c("tc", 0, 512), AF.Copy)
+        for J in range(1, 4):
+            if t and J == 2:
+                repeat(2)
+            tt(c("mx", 2048 * J, 2048 * J + 2048), ind(c("tab", 0, 8192), c(lt, 128 * J, 128 * J + 128)),
+               c("rep", 2048 * J, 2048 * J + 2048), A.max)
+        for h in range(2):
+            for i in range(16):
+                o = c("p%d" % (4 + i // 4), 128 * (i % 4) + 64 * h, 128 * (i % 4) + 64 * h + 64)
+                mm(o, c("iib", 0, 128), c("mx", 1024 * h + i, 1024 * h + 1024, 16), True, False)
+                mm(o, c("nib", 0, 128), c("sw", 64 * h, 64 * h + 64), False, True)
+            gains(1 + h)
+        for b in range(4):
+            act(c("rep", 512 * b, 512 * b + 512), c("p%d" % (4 + b), 0, 512), AF.Relu)
+        gains(0)
+        gains(3)
+        for pb, o, a, b in (("p0", 0, 0, 384), ("p1", 0, 384, 512)):
+            gp = c(pb, o, o + b - a)
+            scan(c("k1", a, b), c("ag", a, b), gp, 0.0, A.add, A.max)
+            tt(c("rec", a, b), gp, c("k1", a, b), A.is_equal)
+            act(c("zz", a, b), gp, AF.Relu, bias=ONE, scale=-1.0)
+            tt(c("rec", a, b), c("p2", a, b), c("rec", a, b), A.mult)
+            scan(c("k2", a, b), c("rs", a, b), c("rec", a, b), 0.0, A.mult, A.max)
+        ti = c("di", 160, 192)
+        cp(ti, c("k2", 15, 512, 16))
+        call, sc1, loc, yb, rem, thr, th, c2, c4, c5, kk1, x1, e1, u1, idx, c1 = [sm(k) for k in range(16)]
+        ts(call, c("k1", 15, 512, 16), 16.0, A.is_ge)
+        ts(c("di", 32, 64), ti, 10, A.arith_shift_right, 7, A.bitwise_and)
+        ts(c("di", 96, 128), ti, 4, A.arith_shift_right, 63, A.bitwise_and)
+        ts(sc1, c("di", 32, 64), 1.0, A.add)
+        ts(c("di", 64, 96), ti, 15, A.bitwise_and)
+        tt(sc1, sc1, call, A.mult)
+        ts(c("di", 0, 32), ti, 1023, A.bitwise_and)
+        for s in range(8):
+            ts(c("oh", s, 256, 8), sc1, float(s + 1), A.is_equal)
+        for J in range(4):
+            mm(c("p4", 64 * J, 64 * J + 64), c("tri", 0, 128), c("oh", 64 * J, 64 * J + 64), True, J == 0)
+            for JJ in range(J):
+                mm(c("p4", 64 * J, 64 * J + 64), c("ones", 0, 128), c("oh", 64 * JJ, 64 * JJ + 64), False, JJ == J - 1)
+        for J in range(4):
+            mm(c("p3", 128 * J, 128 * J + 128), c("zz", 128 * J, 128 * J + 128), c("iib", 0, 128))
+        tt(loc, sc1, c("rn", 0, 32), A.is_equal)
+        tt(c("di", 128, 160), c("di", 32, 64), c("rni", 0, 32), A.subtract)
+        ts(yb, loc, 100.0, A.mult, -100.0, A.add)
+        ts(c("di", 128, 160), c("di", 128, 160), 7, A.bitwise_and)
+        tt(yb, yb, c("di", 96, 128), A.subtract)
+        cp(c("df", 0, 160), c("di", 0, 160))
+        uf, sf, xf, yf, dfl = [c("df", 32 * k, 32 * k + 32) for k in range(5)]
+        for n in range(32):
+            act(c("dl", 64 * n, 64 * n + 64), c("iob", 0, 64), AF.Abs, bias=c("sm", 32 * 3 + n))
+        act(c("bl", 0, 2048), c("dl", 0, 2048), AF.Relu, bias=c("wcol", 6), scale=NW)
+        tt(rem, call, loc, A.subtract)
+        tt(c2, loc, xf, A.mult)
+        ts(c4, sf, 16.0, A.mult, 1.0, A.add)
+        tt(c("pm", 0, 256), c("p4", 0, 256), c("oh", 0, 256), A.mult)
+        tt(c4, c4, c2, A.add)
+        scan(c("pn", 0, 256), c("rs8", 0, 256), c("pm", 0, 256), 0.0, A.mult, A.add)
+        ts(x1, xf, 1.0, A.add)
+        cn = c("pn", 7, 256, 8)
+        ts(c("ki", 64, 96), cn, -1.0, A.add)
+        ts(thr, cn, 48.0, A.is_le)
+        ts(c("ki", 0, 32), c("ki", 64, 96), 15, A.bitwise_and)
+        tt(thr, thr, rem, A.mult)
+        ts(c("ki", 32, 64), c("ki", 64, 96), 4, A.arith_shift_right)
+        tt(th, thr, loc, A.add)
+        tt(c1, c("ki", 0, 32), thr, A.mult)
+        ts(kk1, c("ki", 32, 64), 1.0, A.add)
+        tt(c5, c4, c1, A.add)
+        tt(kk1, kk1, thr, A.mult)
+        tt(c5, c5, th, A.mult)
+        for j in range(3):
+            ts(sm(16 + j), kk1, float(j + 1), A.is_equal)
+        for j in range(3):
+            tt(c("bp", j, 288, 9), sm(16 + j), x1, A.mult)
+            tt(c("bp", 3 + j, 288, 9), sm(16 + j), yf, A.mult)
+            tt(c("bp", 6 + j, 288, 9), sm(16 + j), c("mn", 0, 32), A.mult)
+        for r in range(8):
+            for J in range(4):
+                n = 8 * J + r
+                ts(c("aa", 128 * n, 128 * n + 128), c("iob", 1, 129), c("sm", 32 * 9 + n), A.is_equal)
+                mm(c("p5", 9 * r, 9 * r + 9), c("aa", 128 * n, 128 * n + 128), c("bp", 9 * n, 9 * n + 9), J == 0, J == 3)
+        ts(e1, dfl, 48.0, A.mult, 975.0 - 1360.0, A.add)
+        ts(u1, uf, -1360.0, A.add)
+        tt(e1, e1, cn, A.add)
+        tt(u1, u1, loc, A.mult)
+        cp(("cps", S[:]), c("p5", 0, 72))
+        tt(e1, e1, thr, A.mult)
+        X1, YR, MR = ("cps", S[:, :, 0:3]), ("cps", S[:, :, 3:6]), ("cps", S[:, :, 6:9])
+        cr, c9, ca = sm(20, 24), sm(21, 24), sm(22, 24)
+        ts(cr, X1, 0.0, A.is_gt, G16, A.mult)
+        tt(idx, e1, u1, A.add)
+        ts(ca, MR, 2.0, A.mult)
+        tt(cr, cr, X1, A.add)
+        tt(c("um", 32, 56), ca, c("bl24", 0, 24), A.add)
+        ts(c9, YR, 16.0, A.mult, -1.0, A.add)
+        cp(c("lid", 0, 24), c("um", 32, 56))
+        for cc in range(8):
+            act(("ee", S[:, :, :, cc]), idx, AF.Copy, scale=c("m8", cc))
+        for J in range(4):
+            for r in range(8):
+                n = 8 * J + r
+                mm(c("p6", 64 * J, 64 * J + 64), c("aa", 128 * n, 128 * n + 128), c("bl", 64 * n, 64 * n + 64), r == 0, r == 7)
+        act(c("sw", 512, 896), ind(c("tab", 0, 8192), c("lid", 0, 24)), AF.Copy)
+        act(c("idw", 512, 896), ind(c("iw", 0, 8192), c("lid", 0, 24)), AF.Copy)
+        for n in range(24):
+            r, kk, o = n // 3, n % 3, 64 * (n // 6)
+            ts(c("ar", 128 * n, 128 * n + 128), c("iob", 1, 129), c("sm", 32 * 20 + n), A.is_equal)
+            ts(c("bq", 64 * n, 64 * n + 64), c("iob", 0, 64), ("cps", S[:, r, 3 + kk:4 + kk]), A.is_equal, c("wcol", n % 6), A.mult)
+            mm(c("p7", o, o + 64), c("ar", 128 * n, 128 * n + 128), c("bq", 64 * n, 64 * n + 64), n % 6 == 0, n % 6 == 5)
+            if n == 8:
+                tt(c9, c9, X1, A.add)
+            if n == 9:
+                ts(c("um", 0, 24), c9, 0.0, A.max)
+            if n == 10:
+                cp(c("lud", 0, 32), ind(c("um", 0, 32), c("rl", 0, 2)))
+                cp(c("lidd", 0, 32), ind(c("um", 32, 64), c("rl", 0, 2)))
+            if n == 11:
+                ts(c("lc", 0, 256), c("p6", 0, 256), math.exp(16.0), A.min, B ** 32, A.mult)
+                act(c("lg", 256, 512), c("p6", 0, 256), AF.Ln, bias=TINY)
+                act(c("lg", 512, 768), c("lc", 0, 256), AF.Ln, bias=TINY2)
+        for q in range(8):
+            lq = c("lg", 256 + 256 * (q % 2) + 64 * (q // 2), 320 + 256 * (q % 2) + 64 * (q // 2))
+            act(c("es", 256 + 7 - q, 768, 8), lq, AF.Sign, bias=NTHR)
+            ts(c("va", 256 + 7 - q, 768, 8), lq, 1.0 / (2048 * LNB), A.mult, c("cst", q), A.add)
+        act(c("lg", 0, 256), c("p7", 0, 256), AF.Ln, bias=TINY2)
+        scan(c("vs", 256, 768), c("es", 256, 768), c("va", 256, 768), 0.0, A.max, A.min)
+        for q in range(4):
+            act(c("es", 3 - q, 256, 4), c("lg", 64 * q, 64 * q + 64), AF.Sign, bias=NTHR)
+            ts(c("va", 3 - q, 256, 4), c("lg", 64 * q, 64 * q + 64), 1.0 / (2048 * LNB), A.mult, c("cst", 8 + q), A.add)
+        kl, nl, wl, wl2, tl, kr, ch, e2 = [sq(k) for k in range(8)]
+        ts(kl, c("vs", 256 + 7, 768, 8), -2048.0, A.mult)
+        scan(c("vs", 0, 256), c("es", 0, 256), c("va", 0, 256), 0.0, A.max, A.min)
+        act(c("sid", 0, 336), ind(c("iw", 0, 8192), c("lidd", 0, 21)), AF.Copy)
+        act(c("gs", 0, 336), ind(c(ws, 0, 1024), c("lud", 0, 21)), AF.Copy)
+        for r in range(8):
+            mm(c("p4", 0, 32), c("ztf", 112 - 16 * r, 240 - 16 * r), ("ee", S[:, :, r, :]), r == 0, r == 7)
+        turn("p5", "iib", "gs")
+        ts(nl, kl, 511.5, A.is_ge, 384.0, A.mult)
+        ts(tl, kl, 511.5, A.is_ge, G48N, A.mult)
+        ts(kr, c("vs", 3, 256, 4), -2048.0, A.mult)
+        tt(wl, kl, nl, A.add)
+        ts(tl, tl, G48, A.add)
+        ts(e2, kr, 512.0, A.add)
+        tt(ch, kr, tl, A.is_lt)
+        tt(e2, e2, wl, A.subtract)
+        tt(e2, e2, ch, A.mult)
+        tt(e2, e2, wl, A.add)
+        cp(c("qi", 0, 64), e2)
+        cp(c("lk", 0, 64), c("qi", 0, 64))
+        act(c("ww", 0, 1024), ind(c("idw", 0, 912), c("lk", 0, 64)), AF.Copy)
+        act(c(ws, 1024, 1360), c("p5", 0, 336), AF.Copy)
+        tt(c(wn, 0, 1024), ind(c("sw", 0, 912), c("lk", 0, 64)), c(ws, 0, 1024), A.max)
+        ts(c("li", 0, 32), c("p4", 0, 32), 1360.0, A.add)
+        tt(c("fl", 0, 336), ind(c("ww", 0, 1024), c("lud", 0, 21)), c("sid", 0, 336), A.is_equal)
+        turn("p5", "iib", "fl")
+        cp(c("wt", 1 - t, 1024, 2), c(th_, 0, 512))
+        cp(c("gt", 0, 336), ind(c("wt", 0, 1024), c("lud", 0, 21)))
+        turn("p2", "iif", "gt")
+        act(c("p0", 0, 512), c("ww", 1 - t, 1024, 2), AF.Relu, bias=c("rowm", 4 + t), scale=c("rowm", 2 + t))
+        act(c("ww", 1024, 1360), c("p5", 0, 336), AF.Identity, bias=NEG1, scale=16384.0)
+        if t == 0:
+            act(c("p4", 0, 512), c(wn, t, 1024, 2), AF.Copy)
+        act(c("p1", 0, 512), c("ww", 1 - t, 1024, 2), AF.Relu, scale=c("rowm", t))
+        act(c("p6", 0, 512), c("ww", t, 1024, 2), AF.Relu, bias=c("rowm", 4 + t), scale=c("rowm", 2 + t))
+        act(c("wt", 1024, 1360), c("p2", 0, 336), AF.Copy)
+        act(c("p7", 0, 512), c("ww", t, 1024, 2), AF.Relu, scale=c("rowm", t))
+        if t == 1:
+            act(c("p4", 0, 512), c(wn, t, 1024, 2), AF.Copy)
+
+        def secrets():
+            tt(c("xs", 0, 512), ind(c(ws, 0, 1376), c("li", 0, 32)), c("ff", 0, 512), A.mult)
+            tt(c(wn, t, 1024, 2), c("p4", 0, 512), c("xs", 0, 512), A.max)
+
+        def others_dir():
+            tt(c("hn", 0, 512), c("p0", 0, 512), c("wt", 1 - t, 1024, 2), A.mult)
+            tt(c("hn", 0, 512), c("p1", 0, 512), c("hn", 0, 512), A.add)
+            cp(c("un%d" % t, 0, 512), c("hn", 0, 512))
+
+        def callers_dir():
+            tt(c("p3", 0, 512), c("p3", 0, 512), c("ff", 0, 512), A.mult)
+            tt(c("dt", 0, 512), ind(c("wt", 0, 1376), c("li", 0, 32)), c("tc", 0, 512), A.subtract)
+            tt(c("p3", 0, 512), c("p3", 0, 512), c("dt", 0, 512), A.mult)
+            tt(c("hc", 0, 512), c("p3", 0, 512), c("tc", 0, 512), A.add)
+            tt(c("hc", 0, 512), c("p6", 0, 512), c("hc", 0, 512), A.mult)
+            tt(c("hc", 0, 512), c("p7", 0, 512), c("hc", 0, 512), A.add)
+            cp(c("uc%d" % t, 0, 512), c("hc", 0, 512))
+
+        def flags():
+            tt(c("ff", 0, 512), ind(c("ww", 0, 1376), c("li", 0, 32)), c("idw", 0, 512), A.is_ge)
+
+        if t == 0:
+            flags()
+            secrets()
+            others_dir()
+            hand_on("un0", "lt1", "an2")
+            table(1)
+            callers_dir()
+            hand_on("uc0", "th1", "ac2")
+            act(c("idw", 0, 512), c("idw", 0, 512), AF.Identity, bias=ONE)
+            ts(c("bl24", 0, 24), c("bl24", 0, 24), 1.0, A.add)
+        else:
+            others_dir()
+            dma("s", "en", ("eon", S[:]), ("un1", S[:]))
+            dma("s", "oen", ("ein", S[rank]), ("un1", S[mine, :]))
+            flags()
+            callers_dir()
+            dma("s", "ec", ("eoc", S[:]), ("uc1", S[:]))
+            dma("a", "oec", ("eic", S[rank]), ("uc1", S[mine, :]))
+            secrets()
+            dma("s", "es", ("eso", S[:]), c(wn, 0, 1024))
+            dma("a", "oes", ("ysec", S[mine, :]), (wn, S[mine, 0:1024]))
+            swap("eon", "ein", "aen")
+            swap("eoc", "eic", "aec")
+            swap("eso", "esi", "aes")
+            dma("s", "ln", ("yn", S[:]), ("ein", S[:]))
+            dma("s", "lc", ("yc", S[:]), ("eic", S[:]))
+            if rank > 0:
+                dma("a", "ys", ("ysec", S[0:16 * rank, :]), ("esi", S[0:rank]))
+            if rank < N - 1:
+                dma("a", "ys", ("ysec", S[16 * rank + 16:128, :]), ("esi", S[rank + 1:N]))
+            cp(c("tn", 0, 1024, 2), c("yn", 0, 512))
+            cp(c("tn", 1, 1024, 2), c("yc", 0, 512))
+            dma("s", "yt", ("ytel", S[:]), ("tn", S[:]))
+    for sem in sorted(cnt):
+        wait("g", sem, cnt[sem])
+
+
+def rank_program(g, core, T, topo):
+    rank = T.rank_of(core)
+    if rank is not None:
+        program(g, core, T, topo, rank)

@@ -23,29 +23,29 @@ SCRATCH = {
     "so": slots(128, BF), "si": slots(128, BF), "eso": slots(128, BF), "esi": slots(128, BF),
     "toe": slots(64, U16), "too": slots(64, U16), "tie": slots(64, U16), "tio": slots(64, U16),
     "eon": slots(64, U16), "eoc": slots(64, U16), "ein": slots(64, U16), "eic": slots(64, U16),
-    "tab": sb(8192, BF), "rep": sb(8192, BF), "mx": sb(8192, BF), "iw": sb(8192, F32),
+    "tab": sb(8192, BF), "rep": sb(6144, BF), "mx": sb(8192, BF), "iw": sb(8192, F32),
     "ws0": sb(1376, BF), "ws1": sb(1376, BF), "ws2": sb(1024, BF),
     "wt": sb(1376, F32), "ww": sb(1376, F32), "tn": sb(1024, F32), "t32": sb(1024, I32), "tu": sb(1024, U16),
-    "lt0": sb(512, U16), "th0": sb(512, U16), "lt1": sb(512, U16), "th1": sb(512, U16),
-    "un0": sb(512, U16), "uc0": sb(512, U16), "un1": sb(512, U16), "uc1": sb(512, U16), "yn": sb(512, U16), "yc": sb(512, U16),
+    "lt0": sb(512, U16), "th0": sb(512, U16), "lt1": sb(512, U16), "tf1": sb(512, F32),
+    "un0": sb(512, U16), "un1": sb(512, U16), "uc1": sb(512, U16), "yn": sb(512, U16), "yc": sb(512, U16),
     "sw": sb(912, BF), "idw": sb(912, F32), "tp": sb(512, F32), "tc": sb(512, F32),
     "iob": sb(256, BF), "ioa": sb(128, BF), "iog": sb(128, BF), "pi": sb(8, I32), "pc": sb(16, F32),
     "iib": sb(256, BF), "nib": sb(128, BF), "iif": sb(256, F32), "ztf": sb(240, F32), "one8": sb(8, BF), "negb": sb(128, BF),
     "tri": sb(128, BF), "ones": sb(128, BF), "selr": sb(128 * max(NPE, 1), BF), "tile": sb(128, BF), "m8": sb(8, F32),
-    "wrow": sb(128, F32), "wtmp": sb(128, F32), "wz": sb(128, F32), "wcol": sb(8, F32), "cst": sb(12, F32), "off": sb(12, F32),
-    "l0": sb(2, F32), "ag": sb(512, F32), "rs": sb(512, F32), "rs8": sb(256, F32),
+    "wrow": sb(128, F32), "wtmp": sb(128, F32), "wz": sb(128, F32), "wcol": sb(8, F32), "nwc": sb(8, F32),
+    "cst": sb(12, F32), "off": sb(12, F32), "l0": sb(2, F32), "ag": sb(512, F32), "rs": sb(512, F32), "rs8": sb(256, F32),
     "rn": sb(32, F32), "rni": sb(32, I32), "mn": sb(32, F32),
     "bl24": sb(24, F32), "rl": sb(2, U16), "ctmp": sb(16, F32), "ctmi": sb(16, I32), "rowm": sb(8, F32),
     "k1": sb(512, F32), "rec": sb(512, F32), "k2": sb(512, F32), "zz": sb(512, BF),
     "di": sb(192, I32), "df": sb(160, F32), "sm": sb(768, F32), "ki": sb(96, I32),
     "oh": sb(256, BF), "pm": sb(256, F32), "pn": sb(256, F32),
-    "aa": sb(4096, BF), "bp": sb(288, BF), "dl": sb(2048, BF), "bl": sb(2048, BF),
+    "aa": sb(4096, BF), "bp": sb(288, BF), "dl": sb(2048, BF), "bl": sb(2048, BF), "dq": sb(768, BF), "ny": sb(24, F32),
     "ee": sb([4, 8, 8], F32), "li": sb(32, U16), "cps": sb([8, 9], F32),
     "ar": sb(3072, BF), "bq": sb(1536, BF), "um": sb(64, F32), "lud": sb(32, U16), "lidd": sb(32, U16),
     "lid": sb(24, U16), "gs": sb(336, BF), "gt": sb(336, F32), "sid": sb(336, F32), "fl": sb(336, BF),
     "lc": sb(256, F32), "lg": sb(768, F32), "es": sb(768, F32), "va": sb(768, F32), "vs": sb(768, F32),
     "qi": sb(64, I32), "sq": sb(512, F32), "lk": sb(64, U16),
-    "ff": sb(512, F32), "xs": sb(512, BF), "dt": sb(512, F32), "hn": sb(512, F32), "hc": sb(512, F32),
+    "ff": sb(512, F32), "xs": sb(512, BF), "dt": sb(512, F32), "hn": sb(512, F32), "hc0": sb(512, F32), "hc1": sb(512, F32),
 }
 for _k in range(8):
     SCRATCH["p%d" % _k] = ("psum", [128, 512], F32)
@@ -244,14 +244,14 @@ def program(g, core, T, topo, rank):
     iota(c("iw", 0, 8192), [[1, 8192]], 0, 0)
     for sem, name in (("as1", "si"), ("ae1", "tie"), ("ao1", "tio"), ("aes", "esi"), ("aen", "ein"), ("aec", "eic")):
         landed(sem, N - 1, [(name, S[p]) for p in others])
-    for sem, name in (("an2", "lt1"), ("ac2", "th1")):
+    for sem, name in (("an2", "lt1"), ("ac2", "tf1")):
         landed(sem, len(topo.engines(T.cores[(rank - 1) % N], core)), [(name, S[:])])
 
     ts(c("pi", 1), c("pi", 0), 15, A.bitwise_and)
     ts(c("pi", 2), c("pi", 0), 4, A.arith_shift_right)
     cp(c("pc", 0, 3), c("pi", 0, 3))
     P, PA, PG = c("pc", 0), c("pc", 1), c("pc", 2)
-    G16, G48, G48N, G1K, BT, A112, TINY, TINY2, ONE, NTHR, NEG1, NW, NBT = [c("pc", k) for k in range(3, 16)]
+    G16, G48, G48N, G1K, BT, A112, TINY, TINY2, ONE, NTHR, NEG1, NBT = [c("pc", k) for k in range(3, 15)]
     ts(c("tile", 0, 128), c("ioa", 0, 128), PA, A.is_equal)
     ts(c("m8", 0, 8), c("iob", 0, 8), PG, A.is_equal)
     for k in range(NPE):
@@ -288,7 +288,7 @@ def program(g, core, T, topo, rank):
     ms(c("ag", 0, 512), 1.0)
     ms(c("rs", 0, 512), 1.0)
     ms(c("rs8", 0, 256), 1.0)
-    ts(NW, c("wcol", 6), -1.0, A.mult)
+    ts(c("nwc", 0, 7), c("wcol", 0, 7), -1.0, A.mult)
     ms(c("ag", 0, 512, 16), -1048576.0)
     ms(c("rs", 0, 512, 16), 0.0)
     ms(c("rs8", 0, 256, 8), 0.0)
@@ -329,8 +329,10 @@ def program(g, core, T, topo, rank):
         for i in range(16):
             cp(c("rep", 2048 * J + i, 2048 * J + 2048, 16), c("sw", 128 * J, 128 * J + 128))
 
+    place = {0: ("p1", 0), 1: ("p0", 128), 2: ("p0", 256), 3: ("p3", 128)}
+
     def gains(J):
-        pb, o = ("p0", 128 * J) if J < 3 else ("p1", 0)
+        pb, o = place[J]
         if J:
             mm(c(pb, o, o + 128), c("sw", 128 * J, 128 * J + 128), c("negb", 0, 128), True, False)
         for i in range(16):
@@ -347,10 +349,11 @@ def program(g, core, T, topo, rank):
         for r in range(NPE, N):
             for q in range(N):
                 src = ("si", S[r]) if t == 0 else (ws, S[16 * r:16 * r + 16, 0:1024])
-                dma("sa"[n % 2], "tb%d" % t, ("tab", S[16 * q:16 * q + 16, 1024 * r:1024 * r + 1024]), src)
+                dma("sa"[n % 2 if t == 0 else 0], "tb%d" % t, ("tab", S[16 * q:16 * q + 16, 1024 * r:1024 * r + 1024]), src)
                 n += 1
+                if t == 0 and n == 16:
+                    dma("s", "ne", ("lt0", S[:]), ("tie", S[:]))
         if t == 0:
-            dma("s", "ne", ("lt0", S[:]), ("tie", S[:]))
             dma("s", "no", ("th0", S[:]), ("tio", S[:]))
         for k in range(2 * NPE):
             pb = "p%d" % (4 + k % 2)
@@ -366,24 +369,22 @@ def program(g, core, T, topo, rank):
 
     table(0)
     repeat(2)
-    repeat(3)
     for t in range(2):
-        ws, wn, lt, th_ = "ws%d" % t, "ws%d" % (t + 1), "lt%d" % t, "th%d" % t
+        ws, wn, lt, hc = "ws%d" % t, "ws%d" % (t + 1), "lt%d" % t, "hc%d" % t
         ts(c("tp", 0, 512), c(lt, 0, 512), BT, A.add)
         for JJ in range(4):
             mm(c("p2", 128 * JJ, 128 * JJ + 128), c("tp", 128 * JJ, 128 * JJ + 128), c("iif", 0, 128))
         for h in range(2):
             act(c("mx", 1024 * h, 1024 * h + 1024), ind(c("tab", 0, 8192), c(lt, 64 * h, 64 * h + 64)), AF.Copy)
-        if t:
-            for i in range(16):
-                act(c("rep", 6144 + i, 8192, 16), c("sw", 384, 512), AF.Copy)
-        act(c("tc", 0, 512), c("tp", 0, 512), AF.Identity, bias=NBT)
-        act(c("wt", t, 1024, 2), c("tc", 0, 512), AF.Copy)
-        for J in range(1, 4):
+        act(c("p3", 0, 128), c("sw", 384, 512), AF.Copy)
+        act(c("mx", 6144, 8192), ind(c("tab", 0, 8192), c(lt, 384, 512)), AF.Copy)
+        for J in range(1, 3):
             if t and J == 2:
                 repeat(2)
             tt(c("mx", 2048 * J, 2048 * J + 2048), ind(c("tab", 0, 8192), c(lt, 128 * J, 128 * J + 128)),
                c("rep", 2048 * J, 2048 * J + 2048), A.max)
+        for i in range(16):
+            tt(c("mx", 6144 + i, 8192, 16), c("p3", 0, 128), c("mx", 6144 + i, 8192, 16), A.max)
         for h in range(2):
             for i in range(16):
                 o = c("p%d" % (4 + i // 4), 128 * (i % 4) + 64 * h, 128 * (i % 4) + 64 * h + 64)
@@ -392,10 +393,13 @@ def program(g, core, T, topo, rank):
             gains(1 + h)
         for b in range(4):
             act(c("rep", 512 * b, 512 * b + 512), c("p%d" % (4 + b), 0, 512), AF.Relu)
-        gains(0)
-        gains(3)
-        for pb, o, a, b in (("p0", 0, 0, 384), ("p1", 0, 384, 512)):
-            gp = c(pb, o, o + b - a)
+        last = (0, 3) if t else (3, 0)
+        gains(last[0])
+        gains(last[1])
+        act(c("tc", 0, 512), c("tp", 0, 512), AF.Identity, bias=NBT)
+        for J, w in ((1, 256), (last[0], 128), (last[1], 128)):
+            a, b = 128 * J, 128 * J + w
+            gp = c(place[J][0], place[J][1], place[J][1] + w)
             scan(c("k1", a, b), c("ag", a, b), gp, 0.0, A.add, A.max)
             tt(c("rec", a, b), gp, c("k1", a, b), A.is_equal)
             act(c("zz", a, b), gp, AF.Relu, bias=ONE, scale=-1.0)
@@ -428,7 +432,10 @@ def program(g, core, T, topo, rank):
         uf, sf, xf, yf, dfl = [c("df", 32 * k, 32 * k + 32) for k in range(5)]
         for n in range(32):
             act(c("dl", 64 * n, 64 * n + 64), c("iob", 0, 64), AF.Abs, bias=c("sm", 32 * 3 + n))
-        act(c("bl", 0, 2048), c("dl", 0, 2048), AF.Relu, bias=c("wcol", 6), scale=NW)
+        act(c("bl", 0, 2048), c("dl", 0, 2048), AF.Relu, bias=c("wcol", 6), scale=c("nwc", 6))
+        act(c("wt", t, 1024, 2), c("tc", 0, 512), AF.Copy)
+        if t:
+            act(c("wt", 0, 1024, 2), c("tf1", 0, 512), AF.Copy)
         tt(rem, call, loc, A.subtract)
         tt(c2, loc, xf, A.mult)
         ts(c4, sf, 16.0, A.mult, 1.0, A.add)
@@ -467,41 +474,45 @@ def program(g, core, T, topo, rank):
         tt(e1, e1, thr, A.mult)
         X1, YR, MR = ("cps", S[:, :, 0:3]), ("cps", S[:, :, 3:6]), ("cps", S[:, :, 6:9])
         cr, c9, ca = sm(20, 24), sm(21, 24), sm(22, 24)
+        ts(c("ny", 0, 24), YR, -1.0, A.mult)
         ts(cr, X1, 0.0, A.is_gt, G16, A.mult)
+        for n in range(12, 25):
+            if n < 24:
+                act(c("dq", 64 * (n - 12), 64 * (n - 11)), c("iob", 0, 64), AF.Abs, bias=c("ny", n))
+            if n > 12:
+                act(c("bq", 64 * n - 64, 64 * n), c("dq", 64 * (n - 13), 64 * (n - 12)), AF.Relu,
+                    bias=c("wcol", (n - 1) % 6), scale=c("nwc", (n - 1) % 6))
         tt(idx, e1, u1, A.add)
         ts(ca, MR, 2.0, A.mult)
         tt(cr, cr, X1, A.add)
         tt(c("um", 32, 56), ca, c("bl24", 0, 24), A.add)
         ts(c9, YR, 16.0, A.mult, -1.0, A.add)
+        cp(c("lidd", 0, 32), ind(c("um", 32, 64), c("rl", 0, 2)))
         cp(c("lid", 0, 24), c("um", 32, 56))
-        for cc in range(8):
-            act(("ee", S[:, :, :, cc]), idx, AF.Copy, scale=c("m8", cc))
+        act(c("sid", 0, 336), ind(c("iw", 0, 8192), c("lidd", 0, 21)), AF.Copy)
         for J in range(4):
             for r in range(8):
                 n = 8 * J + r
                 mm(c("p6", 64 * J, 64 * J + 64), c("aa", 128 * n, 128 * n + 128), c("bl", 64 * n, 64 * n + 64), r == 0, r == 7)
-        act(c("sw", 512, 896), ind(c("tab", 0, 8192), c("lid", 0, 24)), AF.Copy)
-        act(c("idw", 512, 896), ind(c("iw", 0, 8192), c("lid", 0, 24)), AF.Copy)
         for n in range(24):
             r, kk, o = n // 3, n % 3, 64 * (n // 6)
             ts(c("ar", 128 * n, 128 * n + 128), c("iob", 1, 129), c("sm", 32 * 20 + n), A.is_equal)
-            ts(c("bq", 64 * n, 64 * n + 64), c("iob", 0, 64), ("cps", S[:, r, 3 + kk:4 + kk]), A.is_equal, c("wcol", n % 6), A.mult)
+            if n < 12:
+                ts(c("bq", 64 * n, 64 * n + 64), c("iob", 0, 64), ("cps", S[:, r, 3 + kk:4 + kk]), A.is_equal, c("wcol", n % 6), A.mult)
             mm(c("p7", o, o + 64), c("ar", 128 * n, 128 * n + 128), c("bq", 64 * n, 64 * n + 64), n % 6 == 0, n % 6 == 5)
-            if n == 8:
-                tt(c9, c9, X1, A.add)
             if n == 9:
-                ts(c("um", 0, 24), c9, 0.0, A.max)
-            if n == 10:
-                cp(c("lud", 0, 32), ind(c("um", 0, 32), c("rl", 0, 2)))
-                cp(c("lidd", 0, 32), ind(c("um", 32, 64), c("rl", 0, 2)))
-            if n == 11:
                 ts(c("lc", 0, 256), c("p6", 0, 256), math.exp(16.0), A.min, B ** 32, A.mult)
                 act(c("lg", 256, 512), c("p6", 0, 256), AF.Ln, bias=TINY)
                 act(c("lg", 512, 768), c("lc", 0, 256), AF.Ln, bias=TINY2)
+        tt(c9, c9, X1, A.add)
+        for cc in range(8):
+            ts(("ee", S[:, :, :, cc]), idx, c("m8", cc), A.mult)
+        ts(c("um", 0, 24), c9, 0.0, A.max)
+        cp(c("lud", 0, 32), ind(c("um", 0, 32), c("rl", 0, 2)))
         for q in range(8):
             lq = c("lg", 256 + 256 * (q % 2) + 64 * (q // 2), 320 + 256 * (q % 2) + 64 * (q // 2))
             act(c("es", 256 + 7 - q, 768, 8), lq, AF.Sign, bias=NTHR)
-            ts(c("va", 256 + 7 - q, 768, 8), lq, 1.0 / (2048 * LNB), A.mult, c("cst", q), A.add)
+            act(c("va", 256 + 7 - q, 768, 8), lq, AF.Identity, bias=c("cst", q), scale=1.0 / (2048 * LNB))
         act(c("lg", 0, 256), c("p7", 0, 256), AF.Ln, bias=TINY2)
         scan(c("vs", 256, 768), c("es", 256, 768), c("va", 256, 768), 0.0, A.max, A.min)
         for q in range(4):
@@ -510,11 +521,14 @@ def program(g, core, T, topo, rank):
         kl, nl, wl, wl2, tl, kr, ch, e2 = [sq(k) for k in range(8)]
         ts(kl, c("vs", 256 + 7, 768, 8), -2048.0, A.mult)
         scan(c("vs", 0, 256), c("es", 0, 256), c("va", 0, 256), 0.0, A.max, A.min)
-        act(c("sid", 0, 336), ind(c("iw", 0, 8192), c("lidd", 0, 21)), AF.Copy)
-        act(c("gs", 0, 336), ind(c(ws, 0, 1024), c("lud", 0, 21)), AF.Copy)
+        if t == 0:
+            cp(c("wt", 1, 1024, 2), c("th0", 0, 512))
+        act(c("idw", 512, 896), ind(c("iw", 0, 8192), c("lid", 0, 24)), AF.Copy)
+        act(c("gt", 0, 336), ind(c("wt", 0, 1024), c("lud", 0, 21)), AF.Copy)
+        act(c("sw", 512, 896), ind(c("tab", 0, 8192), c("lid", 0, 24)), AF.Copy)
         for r in range(8):
             mm(c("p4", 0, 32), c("ztf", 112 - 16 * r, 240 - 16 * r), ("ee", S[:, :, r, :]), r == 0, r == 7)
-        turn("p5", "iib", "gs")
+        turn("p2", "iif", "gt")
         ts(nl, kl, 511.5, A.is_ge, 384.0, A.mult)
         ts(tl, kl, 511.5, A.is_ge, G48N, A.mult)
         ts(kr, c("vs", 3, 256, 4), -2048.0, A.mult)
@@ -528,24 +542,23 @@ def program(g, core, T, topo, rank):
         cp(c("qi", 0, 64), e2)
         cp(c("lk", 0, 64), c("qi", 0, 64))
         act(c("ww", 0, 1024), ind(c("idw", 0, 912), c("lk", 0, 64)), AF.Copy)
-        act(c(ws, 1024, 1360), c("p5", 0, 336), AF.Copy)
         tt(c(wn, 0, 1024), ind(c("sw", 0, 912), c("lk", 0, 64)), c(ws, 0, 1024), A.max)
-        ts(c("li", 0, 32), c("p4", 0, 32), 1360.0, A.add)
         tt(c("fl", 0, 336), ind(c("ww", 0, 1024), c("lud", 0, 21)), c("sid", 0, 336), A.is_equal)
         turn("p5", "iib", "fl")
-        cp(c("wt", 1 - t, 1024, 2), c(th_, 0, 512))
-        cp(c("gt", 0, 336), ind(c("wt", 0, 1024), c("lud", 0, 21)))
-        turn("p2", "iif", "gt")
+        ts(c("li", 0, 32), c("p4", 0, 32), 1360.0, A.add)
         act(c("p0", 0, 512), c("ww", 1 - t, 1024, 2), AF.Relu, bias=c("rowm", 4 + t), scale=c("rowm", 2 + t))
-        act(c("ww", 1024, 1360), c("p5", 0, 336), AF.Identity, bias=NEG1, scale=16384.0)
-        if t == 0:
-            act(c("p4", 0, 512), c(wn, t, 1024, 2), AF.Copy)
         act(c("p1", 0, 512), c("ww", 1 - t, 1024, 2), AF.Relu, scale=c("rowm", t))
-        act(c("p6", 0, 512), c("ww", t, 1024, 2), AF.Relu, bias=c("rowm", 4 + t), scale=c("rowm", 2 + t))
-        act(c("wt", 1024, 1360), c("p2", 0, 336), AF.Copy)
-        act(c("p7", 0, 512), c("ww", t, 1024, 2), AF.Relu, scale=c("rowm", t))
-        if t == 1:
-            act(c("p4", 0, 512), c(wn, t, 1024, 2), AF.Copy)
+        act(c("ww", 1024, 1360), c("p5", 0, 336), AF.Identity, bias=NEG1, scale=16384.0)
+        for part in ((0, 1) if t == 0 else (1, 0)):
+            if part == 0:
+                act(c("gs", 0, 336), ind(c(ws, 0, 1024), c("lud", 0, 21)), AF.Copy)
+                turn("p5", "iib", "gs")
+                act(c("p4", 0, 512), c(wn, t, 1024, 2), AF.Copy)
+                act(c(ws, 1024, 1360), c("p5", 0, 336), AF.Copy)
+            else:
+                act(c("wt", 1024, 1360), c("p2", 0, 336), AF.Copy)
+                act(c("p6", 0, 512), c("ww", t, 1024, 2), AF.Relu, bias=c("rowm", 4 + t), scale=c("rowm", 2 + t))
+                act(c("p7", 0, 512), c("ww", t, 1024, 2), AF.Relu, scale=c("rowm", t))
 
         def secrets():
             tt(c("xs", 0, 512), ind(c(ws, 0, 1376), c("li", 0, 32)), c("ff", 0, 512), A.mult)
@@ -560,30 +573,27 @@ def program(g, core, T, topo, rank):
             tt(c("p3", 0, 512), c("p3", 0, 512), c("ff", 0, 512), A.mult)
             tt(c("dt", 0, 512), ind(c("wt", 0, 1376), c("li", 0, 32)), c("tc", 0, 512), A.subtract)
             tt(c("p3", 0, 512), c("p3", 0, 512), c("dt", 0, 512), A.mult)
-            tt(c("hc", 0, 512), c("p3", 0, 512), c("tc", 0, 512), A.add)
-            tt(c("hc", 0, 512), c("p6", 0, 512), c("hc", 0, 512), A.mult)
-            tt(c("hc", 0, 512), c("p7", 0, 512), c("hc", 0, 512), A.add)
-            cp(c("uc%d" % t, 0, 512), c("hc", 0, 512))
+            tt(c(hc, 0, 512), c("p3", 0, 512), c("tc", 0, 512), A.add)
+            tt(c(hc, 0, 512), c("p6", 0, 512), c(hc, 0, 512), A.mult)
+            tt(c(hc, 0, 512), c("p7", 0, 512), c(hc, 0, 512), A.add)
 
-        def flags():
-            tt(c("ff", 0, 512), ind(c("ww", 0, 1376), c("li", 0, 32)), c("idw", 0, 512), A.is_ge)
-
+        others_dir()
         if t == 0:
-            flags()
-            secrets()
-            others_dir()
             hand_on("un0", "lt1", "an2")
+        else:
+            dma("s", "en", ("eon", S[:]), ("un1", S[:]))
+            dma("s", "oen", ("ein", S[rank]), ("un1", S[mine, :]))
+        tt(c("ff", 0, 512), ind(c("ww", 0, 1376), c("li", 0, 32)), c("idw", 0, 512), A.is_ge)
+        if t == 0:
+            secrets()
             table(1)
             callers_dir()
-            hand_on("uc0", "th1", "ac2")
+            hand_on("hc0", "tf1", "ac2")
             act(c("idw", 0, 512), c("idw", 0, 512), AF.Identity, bias=ONE)
             ts(c("bl24", 0, 24), c("bl24", 0, 24), 1.0, A.add)
         else:
-            others_dir()
-            dma("s", "en", ("eon", S[:]), ("un1", S[:]))
-            dma("s", "oen", ("ein", S[rank]), ("un1", S[mine, :]))
-            flags()
             callers_dir()
+            cp(c("uc1", 0, 512), c(hc, 0, 512))
             dma("s", "ec", ("eoc", S[:]), ("uc1", S[:]))
             dma("a", "oec", ("eic", S[rank]), ("uc1", S[mine, :]))
             secrets()

import math
import numpy as np
from concourse.bass import DstId, RemoteDMATransfer
from concourse.mybir import AluOpType, AxisListType, ActivationFunctionType

N = 8
NPE = 4
B = 2.4
LNB = math.log(B)
W0 = math.exp(43.7)
F32, BF, I32, U16 = "float32", "bfloat16", "int32", "uint16"


def sb(cols, dtp):
    return ("sbuf", [128] + (list(cols) if isinstance(cols, (list, tuple)) else [cols]), dtp)


def slots(cols, dtp):
    return ("dram", [N, 128, cols], dtp)


SCRATCH = {
    "so": slots(128, BF), "si": slots(128, BF), "eso": slots(128, BF), "esi": slots(128, BF),
    "toe": slots(64, U16), "too": slots(64, U16), "tie": slots(64, U16), "tio": slots(64, U16),
    "eon": slots(64, U16), "eoc": slots(64, U16), "ein": slots(64, U16), "eic": slots(64, U16),
    "tab": sb(8192, BF), "rep": sb(6144, BF), "mx": sb(8192, BF), "iw": sb(8192, F32),
    "ws0": sb(1376, BF), "ws1": sb(1376, BF), "ws2": sb(1024, BF),
    "wt": sb(1376, F32), "ww": sb(1376, F32), "tn": sb(1024, F32), "t32": sb(1024, I32), "tu": sb(1024, U16),
    "lt0": sb(512, U16), "th0": sb(512, U16), "lt1": sb(512, U16), "tf1": sb(512, F32),
    "un0": sb(512, U16), "un1": sb(512, U16), "uc1": sb(512, U16), "yn": sb(512, U16), "yc": sb(512, U16),
    "sw": sb(912, BF), "idw": sb(912, F32), "tp": sb(512, F32), "tc": sb(512, F32),
    "iob": sb(256, BF), "ioa": sb(128, BF), "iog": sb(128, BF), "pi": sb(8, I32), "pc": sb(16, F32),
    "iib": sb(256, BF), "nib": sb(128, BF), "iif": sb(256, F32), "ztf": sb(240, F32), "one8": sb(8, BF), "negb": sb(128, BF),
    "tri": sb(128, BF), "ones": sb(128, BF), "selr": sb(128 * max(NPE, 1), BF), "tile": sb(128, BF), "m8": sb(8, F32),
    "wrow": sb(128, F32), "wtmp": sb(128, F32), "wz": sb(128, F32), "wcol": sb(8, F32), "nwc": sb(8, F32),
    "cst": sb(12, F32), "off": sb(12, F32), "l0": sb(2, F32), "ag": sb(512, F32), "rs": sb(512, F32), "rs8": sb(256, F32),
    "rn": sb(32, F32), "rni": sb(32, I32), "mn": sb(32, F32),
    "bl24": sb(24, F32), "rl": sb(2, U16), "ctmp": sb(16, F32), "ctmi": sb(16, I32), "rowm": sb(8, F32),
    "k1": sb(512, F32), "rec": sb(512, F32), "k2": sb(512, F32), "zz": sb(512, BF),
    "di": sb(192, I32), "df": sb(160, F32), "sm": sb(768, F32), "ki": sb(96, I32),
    "oh": sb(256, BF), "pm": sb(256, F32), "pn": sb(256, F32),
    "aa": sb(4096, BF), "bp": sb(288, BF), "dl": sb(2048, BF), "bl": sb(2048, BF), "dq": sb(768, BF), "ny": sb(24, F32),
    "ee": sb([4, 8, 8], F32), "li": sb(32, U16), "cps": sb([8, 9], F32),
    "ar": sb(3072, BF), "bq": sb(1536, BF), "um": sb(64, F32), "lud": sb(32, U16), "lidd": sb(32, U16),
    "lid": sb(24, U16), "gs": sb(336, BF), "gt": sb(336, F32), "sid": sb(336, F32), "fl": sb(336, BF),
    "lc": sb(256, F32), "lg": sb(768, F32), "es": sb(768, F32), "va": sb(768, F32), "vs": sb(768, F32),
    "qi": sb(64, I32), "sq": sb(512, F32), "lk": sb(64, U16),
    "ff": sb(512, F32), "xs": sb(512, BF), "dt": sb(512, F32), "hn": sb(512, F32), "hc0": sb(512, F32), "hc1": sb(512, F32),
}
for _k in range(8):
    SCRATCH["p%d" % _k] = ("psum", [128, 512], F32)
SEMAPHORES = ["qv", "qa", "qp", "qg", "ls", "lt", "os", "oe", "oo", "de", "do", "as1", "ae1", "ao1", "sent", "ns", "ne", "no",
              "tb0", "tb1", "an2", "ac2", "es", "en", "ec", "oen", "oec", "aes", "aen", "aec", "ys", "yt", "oes", "ln", "lc"]

A = AluOpType
AF = ActivationFunctionType


def program(g, core, T, topo, rank):
    S = np.s_
    eng = {"v": g.vector, "a": g.scalar, "p": g.tensor, "g": g, "s": g.sync}
    qsem = {"v": "qv", "a": "qa", "p": "qp", "g": "qg"}
    cnt = {}
    seen = {q: {} for q in eng}
    toks = [None]
    wr, rd = {}, {}
    bank = {}

    def shape(name):
        return SCRATCH[name][1] if name in SCRATCH else list(T[name].shape)

    def psum(name):
        return name in SCRATCH and SCRATCH[name][0] == "psum"

    def known(name):
        if name not in wr:
            wr[name] = np.zeros(shape(name), np.int32)
            rd[name] = {}

    def ap(r):
        if not isinstance(r, tuple):
            return r
        if r[0] == "ind":
            return ap(r[1]).indirect(ap(r[2]))
        return T[r[0]][r[1]]

    def flat(rs):
        out = []
        for r in rs:
            if isinstance(r, tuple):
                out += [r[1], r[2]] if r[0] == "ind" else [r]
        return out

    def wait(q, sem, val):
        if seen[q].get(sem, 0) < val:
            eng[q].wait_ge(T.sem[sem], val)
            seen[q][sem] = val

    def deps(q, reads, writes):
        need = set()
        for name, idx in reads + writes:
            known(name)
            if psum(name):
                for q2, tk in bank.get(name, {}).items():
                    if q2 != q:
                        need.add(tk)
                if q == "p":
                    continue
            need.update(np.unique(wr[name][idx]).tolist())
        for name, idx in writes:
            if q == "p":
                continue
            for arr in rd[name].values():
                need.update(np.unique(arr[idx]).tolist())
        best = {}
        for tk in need:
            if tk:
                sem, val = toks[tk]
                best[sem] = max(best.get(sem, 0), cnt[sem] if val is None else val)
        for sem in sorted(best):
            wait(q, sem, best[sem])

    def mark(q, tk, reads, writes):
        for name, idx in reads:
            if q not in rd[name]:
                rd[name][q] = np.zeros(shape(name), np.int32)
            rd[name][q][idx] = tk
        for name, idx in writes:
            wr[name][idx] = tk
        for name, idx in reads + writes:
            if psum(name):
                bank.setdefault(name, {})[q] = tk

    def op(q, fn, outs, ins):
        reads, writes = flat(ins), flat(outs)
        deps(q, reads, writes)
        sem = qsem[q]
        fn().then_inc(T.sem[sem], 1)
        cnt[sem] = cnt.get(sem, 0) + 1
        toks.append((sem, cnt[sem]))
        mark(q, len(toks) - 1, reads, writes)

    def dma(q, sem, out, in_):
        deps(q, [in_], [out])
        eng[q].dma_start(ap(out), ap(in_)).then_inc(T.sem[sem], 16)
        cnt[sem] = cnt.get(sem, 0) + 16
        toks.append((sem, None))
        mark("d" + sem, len(toks) - 1, [in_], [out])

    def landed(sem, n, refs):
        cnt[sem] = n
        toks.append((sem, n))
        for name, idx in refs:
            known(name)
            wr[name][idx] = len(toks) - 1

    def c(name, a, b=None, step=None):
        return (name, S[:, a:(a + 1 if b is None else b):step])

    def ind(win, off):
        return ("ind", win, off)

    def cp(out, in_):
        op("v", lambda: g.vector.tensor_copy(ap(out), ap(in_)), [out], [in_])

    def tt(out, a, b, o):
        op("v", lambda: g.vector.tensor_tensor(ap(out), ap(a), ap(b), o), [out], [a, b])

    def ts(out, a, s1, o1, s2=None, o2=None):
        if o2 is None:
            op("v", lambda: g.vector.tensor_scalar(ap(out), ap(a), ap(s1), None, o1), [out], [a, s1])
        else:
            op("v", lambda: g.vector.tensor_scalar(ap(out), ap(a), ap(s1), ap(s2), o1, o2), [out], [a, s1, s2])

    def scan(out, d0, d1, init, o0, o1):
        op("v", lambda: g.vector.tensor_tensor_scan(ap(out), ap(d0), ap(d1), init, o0, o1), [out], [d0, d1])

    def ms(out, val):
        op("v", lambda: g.vector.memset(ap(out), val), [out], [])

    def red(out, in_):
        op("v", lambda: g.vector.tensor_reduce(ap(out), ap(in_), AxisListType.X, A.add), [out], [in_])

    def act(out, in_, f, bias=None, scale=None):
        kw = {}
        if bias is not None:
            kw["bias"] = ap(bias)
        if scale is not None:
            kw["scale"] = ap(scale)
        op("a", lambda: g.scalar.activation(ap(out), ap(in_), f, **kw), [out], [in_, bias, scale])

    def mm(out, l, r, start=True, stop=True):
        op("p", lambda: g.tensor.matmul(ap(out), ap(l), ap(r), start, stop), [out], [l, r])

    def iota(out, pat, base, cm, small=True):
        if small:
            op("g", lambda: g.iota(ap(out), pat, base, cm, allow_small_or_imprecise_dtypes=True), [out], [])
        else:
            op("g", lambda: g.iota(ap(out), pat, base, cm), [out], [])

    others = [(rank + d) % N for d in range(1, N)]

    def swap(src, dst, rsem):
        deps("g", [(src, S[p]) for p in others], [])
        trs = []
        for k, p in enumerate(others):
            rid, pid = topo.addr(T.cores[p], core)
            trs.append(RemoteDMATransfer(dst_ids=[DstId(rid=rid, pnc=pid)], dma_engine_mask=1 << topo.engines(core, T.cores[p])[k],
                                         remote_sem=T.sem[rsem], src=T[src][p], dst=T[dst][rank]))
        g.remote_dma_fused(trs, local_sem=T.sem.sent)
        cnt["sent"] = cnt.get("sent", 0) + len(trs)

    def hand_on(src, dst, rsem):
        nxt = T.cores[(rank + 1) % N]
        rid, pid = topo.addr(nxt, core)
        deps("g", [(src, S[:])], [])
        g.remote_dma(T[dst][:], T[src][:], T.sem[rsem], T.sem.sent, pid, rid, topo.mask(core, nxt))
        cnt["sent"] += len(topo.engines(core, nxt))

    mine = S[16 * rank:16 * rank + 16]
    dma("s", "ls", ("so", S[:]), ("sec", S[:]))
    dma("a", "lt", ("t32", S[:]), ("tel", S[:]))
    dma("s", "os", ("si", S[rank]), ("sec", S[mine, :]))
    iota(c("pi", 0), [[0, 1]], 0, 1, False)
    iota(c("iob", 0, 256), [[1, 256]], 0, 0)
    iota(c("ioa", 0, 128), [[0, 8], [1, 16]], 0, 0)
    swap("so", "si", "as1")
    cp(c("tu", 0, 512), c("t32", 0, 1024, 2))
    dma("s", "de", ("toe", S[:]), c("tu", 0, 512))
    dma("a", "oe", ("tie", S[rank]), ("tu", S[mine, 0:512]))
    cp(c("tu", 512, 1024), c("t32", 1, 1024, 2))
    dma("s", "do", ("too", S[:]), c("tu", 512, 1024))
    dma("a", "oo", ("tio", S[rank]), ("tu", S[mine, 512:1024]))
    iota(c("iog", 0, 128), [[1, 8], [0, 16]], 0, 0)
    iota(c("rni", 0, 32), [[0, 4], [1, 8]], 0, 0, False)
    iota(c("mn", 0, 32), [[128, 4], [0, 8]], -256, 1)
    iota(c("bl24", 0, 24), [[1024, 8], [0, 3]], 512, 0)
    iota(c("ctmi", 0, 2), [[16, 2]], 0, 0, False)
    iota(c("off", 0, 8), [[128, 4], [32, 2]], 0, 0)
    iota(c("off", 8, 12), [[96, 4]], 0, 0)
    swap("toe", "tie", "ae1")
    swap("too", "tio", "ao1")
    iota(c("idw", 0, 512), [[2, 512]], 0, 0)
    iota(c("iw", 0, 8192), [[1, 8192]], 0, 0)
    for sem, name in (("as1", "si"), ("ae1", "tie"), ("ao1", "tio"), ("aes", "esi"), ("aen", "ein"), ("aec", "eic")):
        landed(sem, N - 1, [(name, S[p]) for p in others])
    for sem, name in (("an2", "lt1"), ("ac2", "tf1")):
        landed(sem, len(topo.engines(T.cores[(rank - 1) % N], core)), [(name, S[:])])

    ts(c("pi", 1), c("pi", 0), 15, A.bitwise_and)
    ts(c("pi", 2), c("pi", 0), 4, A.arith_shift_right)
    cp(c("pc", 0, 3), c("pi", 0, 3))
    P, PA, PG = c("pc", 0), c("pc", 1), c("pc", 2)
    G16, G48, G48N, G1K, BT, A112, TINY, TINY2, ONE, NTHR, NEG1, NBT = [c("pc", k) for k in range(3, 15)]
    ts(c("tile", 0, 128), c("ioa", 0, 128), PA, A.is_equal)
    ts(c("m8", 0, 8), c("iob", 0, 8), PG, A.is_equal)
    for k in range(NPE):
        ts(c("selr", 128 * k, 128 * k + 128), c("tile", 0, 128), c("m8", k), A.mult)
    ts(G16, PG, 16.0, A.mult)
    ts(G48, PG, 48.0, A.mult, -0.5, A.add)
    ts(G48N, PG, -48.0, A.mult, 384.0, A.add)
    ts(G1K, PG, 1024.0, A.mult)
    ts(BT, PA, 8192.0, A.mult, 8192.0, A.add)
    ts(A112, PA, 112.0, A.add)
    ts(NBT, PA, -8192.0, A.mult, -8192.0, A.add)
    ms(TINY, math.exp(-43.0))
    ms(TINY2, 0.6 * W0 / B ** 95)
    ms(ONE, 1.0)
    ms(NTHR, 39.62)
    ms(NEG1, -1.0)
    for h in range(2):
        ts(c("iib", 128 * h, 128 * h + 128), c("iob", 0, 128), P, A.is_equal)
    ts(c("nib", 0, 128), c("iob", 0, 128), P, A.is_equal, -1.0, A.mult)
    cp(c("iif", 0, 256), c("iib", 0, 256))
    ts(c("ztf", 0, 240), c("iob", 0, 240), A112, A.is_equal)
    ts(c("one8", 0, 8), c("m8", 0, 8), 16.0, A.mult)
    ts(c("tri", 0, 128), c("iob", 0, 128), P, A.is_ge)
    ms(c("ones", 0, 128), 1.0)
    ms(c("wtmp", 0, 128), 1.0 / B)
    ms(c("wz", 0, 128), 0.0)
    scan(c("wrow", 0, 128), c("wtmp", 0, 128), c("wz", 0, 128), W0 * B, A.mult, A.add)
    act(c("l0", 0), c("wrow", 0), AF.Ln)
    tt(c("wtmp", 0, 96), c("wrow", 0, 96), c("tile", 0, 96), A.mult)
    tt(c("wz", 0, 128), c("wrow", 0, 128), c("iib", 0, 128), A.mult)
    for j in range(6):
        red(c("wcol", j), c("wtmp", 16 * j, 16 * j + 16))
    red(c("wcol", 6), c("wz", 0, 128))
    ms(c("ag", 0, 512), 1.0)
    ms(c("rs", 0, 512), 1.0)
    ms(c("rs8", 0, 256), 1.0)
    ts(c("nwc", 0, 7), c("wcol", 0, 7), -1.0, A.mult)
    ms(c("ag", 0, 512, 16), -1048576.0)
    ms(c("rs", 0, 512, 16), 0.0)
    ms(c("rs8", 0, 256, 8), 0.0)
    ms(c("idw", 896, 912), -1.0)
    ms(c("sw", 896, 912), 0.0)
    ms(c("ww", 1360, 1376), -1.0)
    ms(c("wt", 1360, 1376), 0.0)
    ms(c("ws0", 1360, 1376), 0.0)
    ms(c("ws1", 1360, 1376), 0.0)
    ms(c("um", 0, 64), 0.0)
    ts(c("rowm", 0, 2), c("iob", 0, 2), PA, A.is_equal)
    ts(c("l0", 1), c("l0", 0), -1.0 / (2048 * LNB), A.mult, -0.32 / 2048, A.add)
    ts(c("rowm", 2, 4), c("rowm", 0, 2), -1.0, A.mult)
    ts(c("negb", 0, 128), c("iog", 0, 128), PG, A.is_equal, -16.0, A.mult)
    ts(c("rowm", 4, 6), c("rowm", 2, 4), 1.0, A.add)
    ts(c("rn", 0, 32), c("rni", 0, 32), 1.0, A.add)
    ts(c("cst", 0, 12), c("off", 0, 12), -1.0 / 2048, A.mult, c("l0", 1), A.add)
    ts(c("ctmp", 0, 2), c("ctmi", 0, 2), PA, A.add, 20.0, A.min)
    ts(c("ctmp", 2, 4), c("ctmp", 0, 2), -1.0, A.add, 1.0 / 3, A.mult)
    cp(c("ctmi", 2, 4), c("ctmp", 2, 4))
    ts(c("ctmp", 4, 6), c("ctmi", 2, 4), -3.0, A.mult)
    tt(c("ctmp", 4, 6), c("ctmp", 4, 6), c("ctmp", 0, 2), A.add)
    ts(c("ctmp", 6, 8), c("ctmi", 2, 4), -1.0, A.mult, 7.0, A.add)
    ts(c("ctmi", 4, 6), c("ctmp", 6, 8), PG, A.add)
    ts(c("ctmi", 6, 8), c("ctmi", 4, 6), 7, A.bitwise_and)
    ts(c("ctmp", 8, 10), c("ctmi", 6, 8), 3.0, A.mult)
    tt(c("ctmp", 8, 10), c("ctmp", 8, 10), c("ctmp", 4, 6), A.add)
    cp(c("rl", 0, 2), c("ctmp", 8, 10))
    ts(c("idw", 0, 512), c("idw", 0, 512), G1K, A.add)

    def sm(k, n=32):
        return c("sm", 32 * k, 32 * k + n)

    def sq(k):
        return c("sq", 64 * k, 64 * k + 64)

    def repeat(J):
        for i in range(16):
            cp(c("rep", 2048 * J + i, 2048 * J + 2048, 16), c("sw", 128 * J, 128 * J + 128))

    place = {0: ("p1", 0), 1: ("p0", 128), 2: ("p0", 256), 3: ("p3", 128)}

    def gains(J):
        pb, o = place[J]
        if J:
            mm(c(pb, o, o + 128), c("sw", 128 * J, 128 * J + 128), c("negb", 0, 128), True, False)
        for i in range(16):
            if J:
                mm(c(pb, o + i, o + 128, 16), c("mx", 2048 * J + i, 2048 * J + 2048, 16), c("one8", 0, 8), False, i == 15)
            else:
                mm(c(pb, i, 128, 16), c("rep", 128 * i, 128 * i + 128), c("one8", 0, 8))

    def table(t):
        ws = "ws%d" % t
        if t == 0:
            dma("s", "ns", c(ws, 0, 1024), ("si", S[:]))
        n = 0
        for r in range(NPE, N):
            for q in range(N):
                src = ("si", S[r]) if t == 0 else (ws, S[16 * r:16 * r + 16, 0:1024])
                dma("sa"[n % 2 if t == 0 else 0], "tb%d" % t, ("tab", S[16 * q:16 * q + 16, 1024 * r:1024 * r + 1024]), src)
                n += 1
                if t == 0 and n == 16:
                    dma("s", "ne", ("lt0", S[:]), ("tie", S[:]))
        if t == 0:
            dma("s", "no", ("th0", S[:]), ("tio", S[:]))
        for k in range(2 * NPE):
            pb = "p%d" % (4 + k % 2)
            mm(c(pb, 0, 512), c("selr", 128 * (k // 2), 128 * (k // 2) + 128), c(ws, 512 * (k % 2), 512 * (k % 2) + 512))
            act(c("tab", 512 * k, 512 * k + 512), c(pb, 0, 512), AF.Copy)
        cp(c("sw", 0, 512), c(ws, t, 1024, 2))
        repeat(1)

    def turn(pb, ident, src):
        for d in range(1, 8):
            o = 48 * (d - 1)
            mm(c(pb, o, o + 48), c(ident, 16 * d, 16 * d + 128), c(src, o, o + 48))

    table(0)
    repeat(2)
    for t in range(2):
        ws, wn, lt, hc = "ws%d" % t, "ws%d" % (t + 1), "lt%d" % t, "hc%d" % t
        ts(c("tp", 0, 512), c(lt, 0, 512), BT, A.add)
        for JJ in range(4):
            mm(c("p2", 128 * JJ, 128 * JJ + 128), c("tp", 128 * JJ, 128 * JJ + 128), c("iif", 0, 128))
        for h in range(2):
            act(c("mx", 1024 * h, 1024 * h + 1024), ind(c("tab", 0, 8192), c(lt, 64 * h, 64 * h + 64)), AF.Copy)
        act(c("p3", 0, 128), c("sw", 384, 512), AF.Copy)
        act(c("mx", 6144, 8192), ind(c("tab", 0, 8192), c(lt, 384, 512)), AF.Copy)
        for J in range(1, 3):
            if t and J == 2:
                repeat(2)
            tt(c("mx", 2048 * J, 2048 * J + 2048), ind(c("tab", 0, 8192), c(lt, 128 * J, 128 * J + 128)),
               c("rep", 2048 * J, 2048 * J + 2048), A.max)
        for i in range(16):
            tt(c("mx", 6144 + i, 8192, 16), c("p3", 0, 128), c("mx", 6144 + i, 8192, 16), A.max)
        for h in range(2):
            for i in range(16):
                o = c("p%d" % (4 + i // 4), 128 * (i % 4) + 64 * h, 128 * (i % 4) + 64 * h + 64)
                mm(o, c("iib", 0, 128), c("mx", 1024 * h + i, 1024 * h + 1024, 16), True, False)
                mm(o, c("nib", 0, 128), c("sw", 64 * h, 64 * h + 64), False, True)
            gains(1 + h)
        for b in range(4):
            act(c("rep", 512 * b, 512 * b + 512), c("p%d" % (4 + b), 0, 512), AF.Relu)
        last = (0, 3) if t else (3, 0)
        gains(last[0])
        gains(last[1])
        act(c("tc", 0, 512), c("tp", 0, 512), AF.Identity, bias=NBT)
        for J, w in ((1, 256), (last[0], 128), (last[1], 128)):
            a, b = 128 * J, 128 * J + w
            gp = c(place[J][0], place[J][1], place[J][1] + w)
            scan(c("k1", a, b), c("ag", a, b), gp, 0.0, A.add, A.max)
            tt(c("rec", a, b), gp, c("k1", a, b), A.is_equal)
            act(c("zz", a, b), gp, AF.Relu, bias=ONE, scale=-1.0)
            tt(c("rec", a, b), c("p2", a, b), c("rec", a, b), A.mult)
            scan(c("k2", a, b), c("rs", a, b), c("rec", a, b), 0.0, A.mult, A.max)
        ti = c("di", 160, 192)
        cp(ti, c("k2", 15, 512, 16))
        call, sc1, loc, yb, rem, thr, th, c2, c4, c5, kk1, x1, e1, u1, idx, c1 = [sm(k) for k in range(16)]
        ts(call, c("k1", 15, 512, 16), 16.0, A.is_ge)
        ts(c("di", 32, 64), ti, 10, A.arith_shift_right, 7, A.bitwise_and)
        ts(c("di", 96, 128), ti, 4, A.arith_shift_right, 63, A.bitwise_and)
        ts(sc1, c("di", 32, 64), 1.0, A.add)
        ts(c("di", 64, 96), ti, 15, A.bitwise_and)
        tt(sc1, sc1, call, A.mult)
        ts(c("di", 0, 32), ti, 1023, A.bitwise_and)
        for s in range(8):
            ts(c("oh", s, 256, 8), sc1, float(s + 1), A.is_equal)
        for J in range(4):
            mm(c("p4", 64 * J, 64 * J + 64), c("tri", 0, 128), c("oh", 64 * J, 64 * J + 64), True, J == 0)
            for JJ in range(J):
                mm(c("p4", 64 * J, 64 * J + 64), c("ones", 0, 128), c("oh", 64 * JJ, 64 * JJ + 64), False, JJ == J - 1)
        for J in range(4):
            mm(c("p3", 128 * J, 128 * J + 128), c("zz", 128 * J, 128 * J + 128), c("iib", 0, 128))
        tt(loc, sc1, c("rn", 0, 32), A.is_equal)
        tt(c("di", 128, 160), c("di", 32, 64), c("rni", 0, 32), A.subtract)
        ts(yb, loc, 100.0, A.mult, -100.0, A.add)
        ts(c("di", 128, 160), c("di", 128, 160), 7, A.bitwise_and)
        tt(yb, yb, c("di", 96, 128), A.subtract)
        cp(c("df", 0, 160), c("di", 0, 160))
        uf, sf, xf, yf, dfl = [c("df", 32 * k, 32 * k + 32) for k in range(5)]
        for n in range(32):
            act(c("dl", 64 * n, 64 * n + 64), c("iob", 0, 64), AF.Abs, bias=c("sm", 32 * 3 + n))
        act(c("bl", 0, 2048), c("dl", 0, 2048), AF.Relu, bias=c("wcol", 6), scale=c("nwc", 6))
        act(c("wt", t, 1024, 2), c("tc", 0, 512), AF.Copy)
        if t:
            act(c("wt", 0, 1024, 2), c("tf1", 0, 512), AF.Copy)
        tt(rem, call, loc, A.subtract)
        tt(c2, loc, xf, A.mult)
        ts(c4, sf, 16.0, A.mult, 1.0, A.add)
        tt(c("pm", 0, 256), c("p4", 0, 256), c("oh", 0, 256), A.mult)
        tt(c4, c4, c2, A.add)
        scan(c("pn", 0, 256), c("rs8", 0, 256), c("pm", 0, 256), 0.0, A.mult, A.add)
        ts(x1, xf, 1.0, A.add)
        cn = c("pn", 7, 256, 8)
        ts(c("ki", 64, 96), cn, -1.0, A.add)
        ts(thr, cn, 48.0, A.is_le)
        ts(c("ki", 0, 32), c("ki", 64, 96), 15, A.bitwise_and)
        tt(thr, thr, rem, A.mult)
        ts(c("ki", 32, 64), c("ki", 64, 96), 4, A.arith_shift_right)
        tt(th, thr, loc, A.add)
        tt(c1, c("ki", 0, 32), thr, A.mult)
        ts(kk1, c("ki", 32, 64), 1.0, A.add)
        tt(c5, c4, c1, A.add)
        tt(kk1, kk1, thr, A.mult)
        tt(c5, c5, th, A.mult)
        for j in range(3):
            ts(sm(16 + j), kk1, float(j + 1), A.is_equal)
        for j in range(3):
            tt(c("bp", j, 288, 9), sm(16 + j), x1, A.mult)
            tt(c("bp", 3 + j, 288, 9), sm(16 + j), yf, A.mult)
            tt(c("bp", 6 + j, 288, 9), sm(16 + j), c("mn", 0, 32), A.mult)
        for r in range(8):
            for J in range(4):
                n = 8 * J + r
                ts(c("aa", 128 * n, 128 * n + 128), c("iob", 1, 129), c("sm", 32 * 9 + n), A.is_equal)
                mm(c("p5", 9 * r, 9 * r + 9), c("aa", 128 * n, 128 * n + 128), c("bp", 9 * n, 9 * n + 9), J == 0, J == 3)
        ts(e1, dfl, 48.0, A.mult, 975.0 - 1360.0, A.add)
        ts(u1, uf, -1360.0, A.add)
        tt(e1, e1, cn, A.add)
        tt(u1, u1, loc, A.mult)
        cp(("cps", S[:]), c("p5", 0, 72))
        tt(e1, e1, thr, A.mult)
        X1, YR, MR = ("cps", S[:, :, 0:3]), ("cps", S[:, :, 3:6]), ("cps", S[:, :, 6:9])
        cr, c9, ca = sm(20, 24), sm(21, 24), sm(22, 24)
        ts(c("ny", 0, 24), YR, -1.0, A.mult)
        ts(cr, X1, 0.0, A.is_gt, G16, A.mult)
        for n in range(12, 25):
            if n < 24:
                act(c("dq", 64 * (n - 12), 64 * (n - 11)), c("iob", 0, 64), AF.Abs, bias=c("ny", n))
            if n > 12:
                act(c("bq", 64 * n - 64, 64 * n), c("dq", 64 * (n - 13), 64 * (n - 12)), AF.Relu,
                    bias=c("wcol", (n - 1) % 6), scale=c("nwc", (n - 1) % 6))
        tt(idx, e1, u1, A.add)
        ts(ca, MR, 2.0, A.mult)
        tt(cr, cr, X1, A.add)
        tt(c("um", 32, 56), ca, c("bl24", 0, 24), A.add)
        ts(c9, YR, 16.0, A.mult, -1.0, A.add)
        cp(c("lidd", 0, 32), ind(c("um", 32, 64), c("rl", 0, 2)))
        cp(c("lid", 0, 24), c("um", 32, 56))
        act(c("sid", 0, 336), ind(c("iw", 0, 8192), c("lidd", 0, 21)), AF.Copy)
        for J in range(4):
            for r in range(8):
                n = 8 * J + r
                mm(c("p6", 64 * J, 64 * J + 64), c("aa", 128 * n, 128 * n + 128), c("bl", 64 * n, 64 * n + 64), r == 0, r == 7)
        for n in range(24):
            r, kk, o = n // 3, n % 3, 64 * (n // 6)
            ts(c("ar", 128 * n, 128 * n + 128), c("iob", 1, 129), c("sm", 32 * 20 + n), A.is_equal)
            if n < 12:
                ts(c("bq", 64 * n, 64 * n + 64), c("iob", 0, 64), ("cps", S[:, r, 3 + kk:4 + kk]), A.is_equal, c("wcol", n % 6), A.mult)
            mm(c("p7", o, o + 64), c("ar", 128 * n, 128 * n + 128), c("bq", 64 * n, 64 * n + 64), n % 6 == 0, n % 6 == 5)
            if n == 9:
                ts(c("lc", 0, 256), c("p6", 0, 256), math.exp(16.0), A.min, B ** 32, A.mult)
                act(c("lg", 256, 512), c("p6", 0, 256), AF.Ln, bias=TINY)
                act(c("lg", 512, 768), c("lc", 0, 256), AF.Ln, bias=TINY2)
        tt(c9, c9, X1, A.add)
        for cc in range(8):
            ts(("ee", S[:, :, :, cc]), idx, c("m8", cc), A.mult)
        ts(c("um", 0, 24), c9, 0.0, A.max)
        cp(c("lud", 0, 32), ind(c("um", 0, 32), c("rl", 0, 2)))
        for q in range(8):
            lq = c("lg", 256 + 256 * (q % 2) + 64 * (q // 2), 320 + 256 * (q % 2) + 64 * (q // 2))
            act(c("es", 256 + 7 - q, 768, 8), lq, AF.Sign, bias=NTHR)
            act(c("va", 256 + 7 - q, 768, 8), lq, AF.Identity, bias=c("cst", q), scale=1.0 / (2048 * LNB))
        act(c("lg", 0, 256), c("p7", 0, 256), AF.Ln, bias=TINY2)
        scan(c("vs", 256, 768), c("es", 256, 768), c("va", 256, 768), 0.0, A.max, A.min)
        for q in range(4):
            act(c("es", 3 - q, 256, 4), c("lg", 64 * q, 64 * q + 64), AF.Sign, bias=NTHR)
            ts(c("va", 3 - q, 256, 4), c("lg", 64 * q, 64 * q + 64), 1.0 / (2048 * LNB), A.mult, c("cst", 8 + q), A.add)
        kl, nl, wl, wl2, tl, kr, ch, e2 = [sq(k) for k in range(8)]
        ts(kl, c("vs", 256 + 7, 768, 8), -2048.0, A.mult)
        scan(c("vs", 0, 256), c("es", 0, 256), c("va", 0, 256), 0.0, A.max, A.min)
        if t == 0:
            cp(c("wt", 1, 1024, 2), c("th0", 0, 512))
        act(c("idw", 512, 896), ind(c("iw", 0, 8192), c("lid", 0, 24)), AF.Copy)
        act(c("gt", 0, 336), ind(c("wt", 0, 1024), c("lud", 0, 21)), AF.Copy)
        act(c("sw", 512, 896), ind(c("tab", 0, 8192), c("lid", 0, 24)), AF.Copy)
        for r in range(8):
            mm(c("p4", 0, 32), c("ztf", 112 - 16 * r, 240 - 16 * r), ("ee", S[:, :, r, :]), r == 0, r == 7)
        turn("p2", "iif", "gt")
        ts(nl, kl, 511.5, A.is_ge, 384.0, A.mult)
        ts(tl, kl, 511.5, A.is_ge, G48N, A.mult)
        ts(kr, c("vs", 3, 256, 4), -2048.0, A.mult)
        tt(wl, kl, nl, A.add)
        ts(tl, tl, G48, A.add)
        ts(e2, kr, 512.0, A.add)
        tt(ch, kr, tl, A.is_lt)
        tt(e2, e2, wl, A.subtract)
        tt(e2, e2, ch, A.mult)
        tt(e2, e2, wl, A.add)
        cp(c("qi", 0, 64), e2)
        cp(c("lk", 0, 64), c("qi", 0, 64))
        act(c("ww", 0, 1024), ind(c("idw", 0, 912), c("lk", 0, 64)), AF.Copy)
        tt(c(wn, 0, 1024), ind(c("sw", 0, 912), c("lk", 0, 64)), c(ws, 0, 1024), A.max)
        tt(c("fl", 0, 336), ind(c("ww", 0, 1024), c("lud", 0, 21)), c("sid", 0, 336), A.is_equal)
        turn("p5", "iib", "fl")
        ts(c("li", 0, 32), c("p4", 0, 32), 1360.0, A.add)
        act(c("p0", 0, 512), c("ww", 1 - t, 1024, 2), AF.Relu, bias=c("rowm", 4 + t), scale=c("rowm", 2 + t))
        act(c("p1", 0, 512), c("ww", 1 - t, 1024, 2), AF.Relu, scale=c("rowm", t))
        act(c("ww", 1024, 1360), c("p5", 0, 336), AF.Identity, bias=NEG1, scale=16384.0)
        for part in ((0, 1) if t == 0 else (1, 0)):
            if part == 0:
                act(c("gs", 0, 336), ind(c(ws, 0, 1024), c("lud", 0, 21)), AF.Copy)
                turn("p5", "iib", "gs")
                act(c("p4", 0, 512), c(wn, t, 1024, 2), AF.Copy)
                act(c(ws, 1024, 1360), c("p5", 0, 336), AF.Copy)
            else:
                act(c("wt", 1024, 1360), c("p2", 0, 336), AF.Copy)
                act(c("p6", 0, 512), c("ww", t, 1024, 2), AF.Relu, bias=c("rowm", 4 + t), scale=c("rowm", 2 + t))
                act(c("p7", 0, 512), c("ww", t, 1024, 2), AF.Relu, scale=c("rowm", t))

        def secrets():
            tt(c("xs", 0, 512), ind(c(ws, 0, 1376), c("li", 0, 32)), c("ff", 0, 512), A.mult)
            tt(c(wn, t, 1024, 2), c("p4", 0, 512), c("xs", 0, 512), A.max)

        def others_dir():
            tt(c("hn", 0, 512), c("p0", 0, 512), c("wt", 1 - t, 1024, 2), A.mult)
            tt(c("hn", 0, 512), c("p1", 0, 512), c("hn", 0, 512), A.add)
            cp(c("un%d" % t, 0, 512), c("hn", 0, 512))

        def callers_dir():
            tt(c("p3", 0, 512), c("p3", 0, 512), c("ff", 0, 512), A.mult)
            tt(c("dt", 0, 512), ind(c("wt", 0, 1376), c("li", 0, 32)), c("tc", 0, 512), A.subtract)
            tt(c("p3", 0, 512), c("p3", 0, 512), c("dt", 0, 512), A.mult)
            tt(c(hc, 0, 512), c("p3", 0, 512), c("tc", 0, 512), A.add)
            tt(c(hc, 0, 512), c("p6", 0, 512), c(hc, 0, 512), A.mult)
            tt(c(hc, 0, 512), c("p7", 0, 512), c(hc, 0, 512), A.add)

        others_dir()
        if t == 0:
            hand_on("un0", "lt1", "an2")
        else:
            dma("s", "en", ("eon", S[:]), ("un1", S[:]))
            dma("s", "oen", ("ein", S[rank]), ("un1", S[mine, :]))
        tt(c("ff", 0, 512), ind(c("ww", 0, 1376), c("li", 0, 32)), c("idw", 0, 512), A.is_ge)
        if t == 0:
            secrets()
            table(1)
            callers_dir()
            hand_on("hc0", "tf1", "ac2")
            act(c("idw", 0, 512), c("idw", 0, 512), AF.Identity, bias=ONE)
            ts(c("bl24", 0, 24), c("bl24", 0, 24), 1.0, A.add)
        else:
            callers_dir()
            cp(c("uc1", 0, 512), c(hc, 0, 512))
            dma("s", "ec", ("eoc", S[:]), ("uc1", S[:]))
            dma("a", "oec", ("eic", S[rank]), ("uc1", S[mine, :]))
            secrets()
            dma("s", "es", ("eso", S[:]), c(wn, 0, 1024))
            dma("a", "oes", ("ysec", S[mine, :]), (wn, S[mine, 0:1024]))
            swap("eon", "ein", "aen")
            swap("eoc", "eic", "aec")
            swap("eso", "esi", "aes")
            dma("s", "ln", ("yn", S[:]), ("ein", S[:]))
            dma("s", "lc", ("yc", S[:]), ("eic", S[:]))
            if rank > 0:
                dma("a", "ys", ("ysec", S[0:16 * rank, :]), ("esi", S[0:rank]))
            if rank < N - 1:
                dma("a", "ys", ("ysec", S[16 * rank + 16:128, :]), ("esi", S[rank + 1:N]))
            cp(c("tn", 0, 1024, 2), c("yn", 0, 512))
            cp(c("tn", 1, 1024, 2), c("yc", 0, 512))
            dma("s", "yt", ("ytel", S[:]), ("tn", S[:]))
    for sem in sorted(cnt):
        wait("g", sem, cnt[sem])


def rank_program(g, core, T, topo):
    rank = T.rank_of(core)
    if rank is not None:
        program(g, core, T, topo, rank)
